import numpy as np
import ml_dtypes


def mxq(x, axis, fmt="e4m3"):
    dtype, down = {"e4m3": (ml_dtypes.float8_e4m3fn, 7), "e5m2": (ml_dtypes.float8_e5m2, 14)}[fmt]
    v = np.moveaxis(np.asarray(x, np.float32).astype(ml_dtypes.bfloat16).astype(np.float64), axis, -1)
    blocks = v.reshape(v.shape[:-1] + (-1, 32))
    amax = np.abs(blocks).max(-1, keepdims=True)
    byte = np.maximum(np.where(amax > 0, np.frexp(amax)[1] - 1 + 127, 0) - down, 1)
    scale = np.exp2(byte - 127.0)
    codes = (blocks / scale).astype(np.float32).astype(dtype).astype(np.float64)
    return np.moveaxis((codes * scale).reshape(v.shape), -1, axis)


WIDE = False


def mx_kscale(k):
    if not WIDE:
        return np.ones(k)
    levels = np.array([10, -10, 5, -5, 0])
    if k % 512:
        return np.exp2(np.random.permutation(np.resize(levels, k // 32))).repeat(32)
    a = np.empty((k // 512, 16))
    for p in range(k // 512):
        a[p, :8] = np.random.permutation(np.resize(levels, 8))
        for g in range(8):
            far = levels[np.abs(levels - a[p, g]) >= 10]
            a[p, g + 8] = far[np.random.randint(len(far))]
    return np.exp2(a.ravel()).repeat(32)


def f64(x):
    return np.asarray(x).astype(np.float64)


def striped8(idx):
    return np.concatenate([v.reshape(-1, 16).T for v in idx]).astype(np.uint16)


def unstriped8(offs):
    return np.stack([offs[16 * g:16 * g + 16].T.reshape(-1) for g in range(8)]).astype(np.int64)


E2M1 = np.array([0.0, 0.5, 1.0, 1.5, 2.0, 3.0, 4.0, 6.0, -0.0, -0.5, -1.0, -1.5, -2.0, -3.0, -4.0, -6.0])


def pack_weight(w, fmt):
    k, n = w.shape
    w = f64(np.asarray(w, np.float32).astype(ml_dtypes.bfloat16)).reshape(k // 32, 32, n)
    amax = np.abs(w).max(1)
    if fmt == "e4m3":
        byte = np.frexp(amax)[1] - 1 + 127 - 7
    else:
        mant, ex = np.frexp(amax / 6.0)
        byte = np.where(mant > 0.5, ex, ex - 1) + 127
    byte = np.clip(np.where(amax > 0, byte, 1), 1, 254)
    scaled = (w * np.exp2(127.0 - byte)[:, None, :]).reshape(k, n).astype(np.float32)
    by_word = np.ascontiguousarray(scaled.reshape(k // 512, 128, 4, n).transpose(0, 1, 3, 2))
    if fmt == "e4m3":
        words = by_word.astype(ml_dtypes.float8_e4m3fn).view(np.uint8)
    else:
        c = by_word.astype(ml_dtypes.float4_e2m1fn).view(np.uint8) & 0xF
        words = (c[..., 0::2] | (c[..., 1::2] << 4)).reshape(k // 512, 128, 2 * n)
    return np.ascontiguousarray(words), np.ascontiguousarray(byte.astype(np.uint8).reshape(k // 512, 16, n))


def unpack_weight(words, scales, fmt):
    g, _, n = scales.shape
    words = np.ascontiguousarray(words).reshape(g, 128, n, -1)
    if fmt == "e4m3":
        vals = words.view(ml_dtypes.float8_e4m3fn).astype(np.float64)
    else:
        nib = np.empty((g, 128, n, 4), np.uint8)
        nib[..., 0::2] = words & 0xF
        nib[..., 1::2] = words >> 4
        vals = E2M1[nib]
    vals = vals * np.repeat(np.exp2(scales.astype(np.float64) - 127.0), 8, axis=1)[..., None]
    return vals.transpose(0, 1, 3, 2).reshape(g * 512, n)


K, M, T, S = 1536, 128, 1024, 512


def setup_inputs():
    n = np.random.standard_normal
    s = mx_kscale(K)[:, None]
    w = n((K, M)) / np.sqrt(K) / s
    w4 = pack_weight(w, "e2m1")
    rest = w - unpack_weight(*w4, "e2m1")
    p_r8 = pack_weight(rest, "e4m3")
    return {
        "xT": (n((K, T)) * s).astype(np.float32),
        "w4_words": w4[0],
        "w4_scales": w4[1],
        "r8_words": p_r8[0],
        "r8_scales": p_r8[1],
        "wgt": np.repeat(np.random.uniform(0.5, 2.0, (8, S)), 16, axis=0).astype(np.float32),
        "wgo": np.repeat(np.random.uniform(0.5, 2.0, (8, S)), 16, axis=0).astype(np.float32),
        "offs": striped8(np.stack([np.random.permutation(T)[:S] for _ in range(8)])),
        "offs2": striped8(np.stack([np.random.permutation(T)[:S] for _ in range(8)])),
    }


def reference(xT, w4_words, w4_scales, r8_words, r8_scales, wgt, wgo, offs, offs2):
    idx = unstriped8(offs)
    group = np.arange(K) % 512 // 64
    xg = f64(wgt)[np.arange(K) // 4 % 128] * f64(xT)[np.arange(K)[:, None], idx[group]]
    xT_ = mxq(xg, 0, "e4m3")
    w4_ = unpack_weight(w4_words, w4_scales, "e2m1")
    r8_ = unpack_weight(r8_words, r8_scales, "e4m3")
    y = w4_.T @ xT_ + r8_.T @ xT_
    place = unstriped8(offs2)[np.arange(M) % 128 // 16]
    out = np.zeros((M, T))
    out[np.arange(M)[:, None], place] = f64(wgo)[np.arange(M) % 128] * (y)
    return out

@@ -1,0 +1,156 @@
+from contextlib import ExitStack
+
+import concourse.mybir as mybir
+
+K, M, T, S = 1536, 128, 1024, 512
+FLOPS = 2 * 2 * K * M * S
+
+F32 = mybir.dt.float32
+BF16 = mybir.dt.bfloat16
+I32 = mybir.dt.int32
+U32 = mybir.dt.uint32
+U16 = mybir.dt.uint16
+U8 = mybir.dt.uint8
+FP8X4 = mybir.dt.float8_e4m3fn_x4
+FP4X4 = mybir.dt.float4_e2m1fn_x4
+MULT = mybir.AluOpType.mult
+
+P = 128
+PACK = 4
+K_PASS = P * PACK
+PASSES = K // K_PASS
+HALF = S // 2
+N_MM = 128
+LIST_ROWS = 16
+
+
+def tile_list_hboth_none_kernel(
+    tc, xT, w4_words, w4_scales, r8_words, r8_scales, wgt, wgo, offs, offs2, out
+):
+    nc = tc.nc
+    with ExitStack() as ctx:
+        keep = ctx.enter_context(tc.tile_pool(name="keep", bufs=1))
+        psum = ctx.enter_context(tc.psum_pool(name="psum", bufs=1))
+
+        def sb(name, shape, dtype):
+            return keep.tile(shape, dtype, name=name, align_bytes=64)
+
+        gather_list = keep.tile([P, S // LIST_ROWS], U16, name="gather_list")
+        scatter_list = keep.tile([P, S // LIST_ROWS], U16, name="scatter_list")
+        wgt_sb = [sb(f"wgt{h}", [P, HALF], F32) for h in range(2)]
+        wgo_sb = sb("wgo", [P, S], F32)
+        planes = [[sb(f"plane{a}_{i}", [P, T], F32) for i in range(PACK)] for a in range(PASSES)]
+        w4_sb = sb("w4", [P, PASSES, 2 * M], U8)
+        r8_sb = sb("r8", [P, PASSES, PACK * M], U8)
+        w_scale = sb("w_scale", [P, 2, PASSES, M], U8)
+        picked = [[sb(f"picked{a}_{h}", [P, PACK, HALF], F32) for h in range(2)] for a in range(PASSES)]
+        grouped = [[sb(f"grouped{a}_{h}", [P, HALF, PACK], BF16) for h in range(2)] for a in range(PASSES)]
+        codes = [[sb(f"codes{a}_{h}", [P, HALF], U32) for h in range(2)] for a in range(PASSES)]
+        x_scale = [[sb(f"x_scale{a}_{h}", [P, HALF], U8) for h in range(2)] for a in range(PASSES)]
+        y_sb = [sb(f"y{h}", [P, HALF], F32) for h in range(2)]
+        out_sb = sb("out_sb", [P, T], F32)
+        acc = [[psum.tile([P, N_MM], F32, name=f"acc{h}_{q}") for q in range(2)] for h in range(2)]
+
+        nc.vector.memset(w_scale[:].rearrange("p w a n -> p (w a n)").bitcast(I32), 0)
+        nc.vector.memset(out_sb[:], 0.0)
+
+        def load_plane(a, i):
+            rows = xT[a * K_PASS : (a + 1) * K_PASS, :].rearrange("(p i) t -> p i t", i=PACK)
+            nc.sync.dma_start(out=planes[a][i][:], in_=rows[:, i, :])
+
+        nc.sync.dma_start(gather_list[:], offs)
+        nc.sync.dma_start(out=wgt_sb[0][:], in_=wgt[:, :HALF])
+        load_plane(0, 0)
+        nc.sync.dma_start(out=wgt_sb[1][:], in_=wgt[:, HALF:])
+        for n in range(1, PASSES * PACK):
+            load_plane(n // PACK, n % PACK)
+        nc.sync.dma_start(out=w4_sb[:].bitcast(I32), in_=w4_words.rearrange("a p n -> p a n").bitcast(I32))
+        nc.sync.dma_start(out=r8_sb[:].bitcast(I32), in_=r8_words.rearrange("a p n i -> p a (n i)").bitcast(I32))
+        nc.sync.dma_start(scatter_list[:], offs2)
+        nc.sync.dma_start(out=wgo_sb[:], in_=wgo)
+        for w, scales in enumerate((w4_scales, r8_scales)):
+            for quad in range(4):
+                nc.gpsimd.dma_start(
+                    out=w_scale[32 * quad : 32 * quad + 4, w].bitcast(I32),
+                    in_=scales[:, 4 * quad : 4 * quad + 4, :].rearrange("a r n -> r a n").bitcast(I32),
+                )
+
+        def list_half(lst, h):
+            cols = HALF // LIST_ROWS
+            return lst[:, h * cols : (h + 1) * cols]
+
+        def gather(a, i, h):
+            nc.vector.tensor_tensor(
+                picked[a][h][:, i, :], planes[a][i][:].indirect(list_half(gather_list, h)), wgt_sb[h][:], MULT
+            )
+
+        def interleave(a, h, first, last):
+            nc.scalar.copy(
+                out=grouped[a][h][:, :, first:last],
+                in_=picked[a][h][:, first:last, :].rearrange("p i c -> p c i"),
+            )
+
+        def quantize(a, h):
+            nc.vector.quantize_mx(
+                out=codes[a][h][:].bitcast(FP8X4),
+                scales=x_scale[a][h][:],
+                in_=grouped[a][h][:].rearrange("p c i -> p (c i)"),
+            )
+
+        def multiply(a, h, start, stop):
+            for q in range(2):
+                cols = slice(q * N_MM, (q + 1) * N_MM)
+                rhs = codes[a][h][:, cols].bitcast(FP8X4)
+                nc.tensor.matmul_mx(
+                    out=acc[h][q][:], lhsT=w4_sb[:, a, :].bitcast(FP4X4), lhsT_scale=w_scale[:, 0, a, :],
+                    rhs=rhs, rhs_scale=x_scale[a][h][:, cols], start=start, stop=False,
+                )
+                nc.tensor.matmul_mx(
+                    out=acc[h][q][:], lhsT=r8_sb[:, a, :].bitcast(FP8X4), lhsT_scale=w_scale[:, 1, a, :],
+                    rhs=rhs, rhs_scale=x_scale[a][h][:, cols], start=False, stop=stop,
+                )
+                if stop:
+                    nc.scalar.copy(out=y_sb[h][:, cols], in_=acc[h][q][:])
+
+        def scatter(h):
+            nc.vector.tensor_tensor(
+                out_sb[:].indirect(list_half(scatter_list, h)), y_sb[h][:], wgo_sb[:, h * HALF : (h + 1) * HALF], MULT
+            )
+
+        def gather_plane(a, i):
+            for h in range(2):
+                gather(a, i, h)
+
+        for i in range(PACK):
+            gather_plane(0, i)
+        for h in range(2):
+            interleave(0, h, 0, PACK)
+        gather_plane(1, 0)
+        gather_plane(1, 1)
+        quantize(0, 0)
+        gather_plane(1, 2)
+        gather_plane(1, 3)
+        for h in range(2):
+            interleave(1, h, 0, PACK)
+        gather_plane(2, 0)
+        gather_plane(2, 1)
+        for h in range(2):
+            interleave(2, h, 0, 2)
+        quantize(1, 0)
+        gather_plane(2, 2)
+        gather_plane(2, 3)
+        for h in range(2):
+            interleave(2, h, 2, PACK)
+        multiply(0, 0, True, False)
+        multiply(1, 0, False, False)
+        quantize(1, 1)
+        quantize(2, 0)
+        multiply(2, 0, False, True)
+        quantize(0, 1)
+        quantize(2, 1)
+        multiply(1, 1, True, False)
+        multiply(0, 1, False, False)
+        multiply(2, 1, False, True)
+        scatter(0)
+        scatter(1)
+        nc.sync.dma_start(out=out, in_=out_sb[:])

@@ -32,21 +32,22 @@ def tile_list_hboth_none_kernel(
         keep = ctx.enter_context(tc.tile_pool(name="keep", bufs=1))
         psum = ctx.enter_context(tc.psum_pool(name="psum", bufs=1))
 
-        def sb(name, shape, dtype):
-            return keep.tile(shape, dtype, name=name, align_bytes=64)
+        def sb(name, shape, dtype, tag=None):
+            return keep.tile(shape, dtype, name=name, tag=tag or name, align_bytes=64)
 
         gather_list = keep.tile([P, S // LIST_ROWS], U16, name="gather_list")
         scatter_list = keep.tile([P, S // LIST_ROWS], U16, name="scatter_list")
-        wgt_sb = [sb(f"wgt{h}", [P, HALF], F32) for h in range(2)]
+        wgt_sb = [sb(f"wgt{h}", [P, HALF], F32) for h in range(3)]
         wgo_sb = sb("wgo", [P, S], F32)
         planes = [[sb(f"plane{a}_{i}", [P, T], F32) for i in range(PACK)] for a in range(PASSES)]
         w4_sb = sb("w4", [P, PASSES, 2 * M], U8)
         r8_sb = sb("r8", [P, PASSES, PACK * M], U8)
         w_scale = sb("w_scale", [P, 2, PASSES, M], U8)
         picked = [[sb(f"picked{a}_{h}", [P, PACK, HALF], F32) for h in range(2)] for a in range(PASSES)]
-        grouped = [[sb(f"grouped{a}_{h}", [P, HALF, PACK], BF16) for h in range(2)] for a in range(PASSES)]
-        codes = [[sb(f"codes{a}_{h}", [P, HALF], U32) for h in range(2)] for a in range(PASSES)]
-        x_scale = [[sb(f"x_scale{a}_{h}", [P, HALF], U8) for h in range(2)] for a in range(PASSES)]
+        early = [sb(f"early{h}", [P, PASSES - 1, HALF, PACK], BF16) for h in range(2)]
+        last_pass = [sb(f"last{h}", [P, 1, HALF, PACK], BF16) for h in range(2)]
+        x_scale = [sb(f"x_scale{h}", [P, PASSES, HALF], U8) for h in range(2)]
+        codes = {}
         y_sb = [sb(f"y{h}", [P, HALF], F32) for h in range(2)]
         out_sb = sb("out_sb", [P, T], F32)
         acc = [[psum.tile([P, N_MM], F32, name=f"acc{h}_{q}") for q in range(2)] for h in range(2)]
@@ -58,12 +59,13 @@ def tile_list_hboth_none_kernel(
             rows = xT[a * K_PASS : (a + 1) * K_PASS, :].rearrange("(p i) t -> p i t", i=PACK)
             nc.sync.dma_start(out=planes[a][i][:], in_=rows[:, i, :])
 
+        load_plane(0, 0)
         nc.sync.dma_start(gather_list[:], offs)
         nc.sync.dma_start(out=wgt_sb[0][:], in_=wgt[:, :HALF])
-        load_plane(0, 0)
         nc.sync.dma_start(out=wgt_sb[1][:], in_=wgt[:, HALF:])
         for n in range(1, PASSES * PACK):
             load_plane(n // PACK, n % PACK)
+        nc.sync.dma_start(out=wgt_sb[2][:], in_=wgt[:, HALF:])
         nc.sync.dma_start(out=w4_sb[:].bitcast(I32), in_=w4_words.rearrange("a p n -> p a n").bitcast(I32))
         nc.sync.dma_start(out=r8_sb[:].bitcast(I32), in_=r8_words.rearrange("a p n i -> p a (n i)").bitcast(I32))
         nc.sync.dma_start(scatter_list[:], offs2)
@@ -75,81 +77,86 @@ def tile_list_hboth_none_kernel(
                     in_=scales[:, 4 * quad : 4 * quad + 4, :].rearrange("a r n -> r a n").bitcast(I32),
                 )
 
-        def list_half(lst, h):
-            cols = HALF // LIST_ROWS
-            return lst[:, h * cols : (h + 1) * cols]
+        def list_part(lst, first, count):
+            return lst[:, first // LIST_ROWS : (first + count) // LIST_ROWS]
 
-        def gather(a, i, h):
-            nc.vector.tensor_tensor(
-                picked[a][h][:, i, :], planes[a][i][:].indirect(list_half(gather_list, h)), wgt_sb[h][:], MULT
-            )
+        def gather(a, i, h, weights, cols=slice(0, HALF)):
+            offsets = list_part(gather_list, h * HALF + cols.start, cols.stop - cols.start)
+            nc.vector.tensor_tensor(picked[a][h][:, i, cols], planes[a][i][:].indirect(offsets), weights, MULT)
 
-        def interleave(a, h, first, last):
+        def interleave(a, h, first, last, cols=slice(0, HALF)):
+            grouped = early[h][:, a] if a < PASSES - 1 else last_pass[h][:, 0]
             nc.scalar.copy(
-                out=grouped[a][h][:, :, first:last],
-                in_=picked[a][h][:, first:last, :].rearrange("p i c -> p c i"),
+                out=grouped[:, cols, first:last],
+                in_=picked[a][h][:, first:last, cols].rearrange("p i c -> p c i"),
             )
 
-        def quantize(a, h):
-            nc.vector.quantize_mx(
-                out=codes[a][h][:].bitcast(FP8X4),
-                scales=x_scale[a][h][:],
-                in_=grouped[a][h][:].rearrange("p c i -> p (c i)"),
-            )
+        def quantize(h, first, last, tag=None, pieces=1):
+            words = sb(f"codes{h}_{first}", [P, last - first, HALF], U32, tag)
+            for a in range(first, last):
+                codes[a, h] = words[:, a - first, :]
+            grouped = early[h] if first == 0 else last_pass[h]
+            width = (last - first) * HALF // pieces
+            for c0 in range(0, (last - first) * HALF, width):
+                cols = slice(c0, c0 + width)
+                nc.vector.quantize_mx(
+                    out=words[:].rearrange("p a c -> p (a c)")[:, cols].bitcast(FP8X4),
+                    scales=x_scale[h][:, first:last, :].rearrange("p a c -> p (a c)")[:, cols],
+                    in_=grouped[:].rearrange("p a c i -> p (a c) i")[:, cols, :].rearrange("p c i -> p (c i)"),
+                )
 
         def multiply(a, h, start, stop):
             for q in range(2):
                 cols = slice(q * N_MM, (q + 1) * N_MM)
-                rhs = codes[a][h][:, cols].bitcast(FP8X4)
+                rhs = codes[a, h][:, cols].bitcast(FP8X4)
                 nc.tensor.matmul_mx(
                     out=acc[h][q][:], lhsT=w4_sb[:, a, :].bitcast(FP4X4), lhsT_scale=w_scale[:, 0, a, :],
-                    rhs=rhs, rhs_scale=x_scale[a][h][:, cols], start=start, stop=False,
+                    rhs=rhs, rhs_scale=x_scale[h][:, a, cols], start=start, stop=False,
                 )
                 nc.tensor.matmul_mx(
                     out=acc[h][q][:], lhsT=r8_sb[:, a, :].bitcast(FP8X4), lhsT_scale=w_scale[:, 1, a, :],
-                    rhs=rhs, rhs_scale=x_scale[a][h][:, cols], start=False, stop=stop,
+                    rhs=rhs, rhs_scale=x_scale[h][:, a, cols], start=False, stop=stop,
                 )
                 if stop:
                     nc.scalar.copy(out=y_sb[h][:, cols], in_=acc[h][q][:])
 
         def scatter(h):
             nc.vector.tensor_tensor(
-                out_sb[:].indirect(list_half(scatter_list, h)), y_sb[h][:], wgo_sb[:, h * HALF : (h + 1) * HALF], MULT
+                out_sb[:].indirect(list_part(scatter_list, h * HALF, HALF)),
+                y_sb[h][:],
+                wgo_sb[:, h * HALF : (h + 1) * HALF],
+                MULT,
             )
 
         def gather_plane(a, i):
             for h in range(2):
-                gather(a, i, h)
+                gather(a, i, h, wgt_sb[h][:])
 
-        for i in range(PACK):
-            gather_plane(0, i)
-        for h in range(2):
-            interleave(0, h, 0, PACK)
-        gather_plane(1, 0)
-        gather_plane(1, 1)
-        quantize(0, 0)
-        gather_plane(1, 2)
-        gather_plane(1, 3)
-        for h in range(2):
-            interleave(1, h, 0, PACK)
+        for a in range(2):
+            for i in range(PACK):
+                gather_plane(a, i)
+            for h in range(2):
+                interleave(a, h, 0, PACK)
         gather_plane(2, 0)
         gather_plane(2, 1)
         for h in range(2):
             interleave(2, h, 0, 2)
-        quantize(1, 0)
-        gather_plane(2, 2)
-        gather_plane(2, 3)
-        for h in range(2):
-            interleave(2, h, 2, PACK)
+        quantize(0, 0, 2)
         multiply(0, 0, True, False)
         multiply(1, 0, False, False)
-        quantize(1, 1)
-        quantize(2, 0)
+        gather(2, 2, 0, wgt_sb[0][:])
+        gather(2, 3, 0, wgt_sb[0][:])
+        interleave(2, 0, 2, PACK)
+        for cols in (slice(0, N_MM), slice(N_MM, HALF)):
+            gather(2, 2, 1, wgt_sb[2][:, cols], cols)
+            gather(2, 3, 1, wgt_sb[2][:, cols], cols)
+            interleave(2, 1, 2, PACK, cols)
+        quantize(0, 2, 3, pieces=2)
         multiply(2, 0, False, True)
-        quantize(0, 1)
-        quantize(2, 1)
-        multiply(1, 1, True, False)
-        multiply(0, 1, False, False)
+        quantize(1, 0, 2, "picked2_0")
+        quantize(1, 2, 3)
+        multiply(0, 1, True, False)
+        multiply(1, 1, False, False)
         multiply(2, 1, False, True)
         scatter(0)
         scatter(1)

@@ -37,13 +37,20 @@ def tile_list_hboth_none_kernel(
 
         gather_list = keep.tile([P, S // LIST_ROWS], U16, name="gather_list")
         scatter_list = keep.tile([P, S // LIST_ROWS], U16, name="scatter_list")
-        wgt_sb = [sb(f"wgt{h}", [P, HALF], F32) for h in range(3)]
+        wgt_sb = [sb(f"wgt{h}", [P, HALF], F32) for h in range(2)]
         wgo_sb = sb("wgo", [P, S], F32)
         planes = [[sb(f"plane{a}_{i}", [P, T], F32) for i in range(PACK)] for a in range(PASSES)]
         w4_sb = sb("w4", [P, PASSES, 2 * M], U8)
         r8_sb = sb("r8", [P, PASSES, PACK * M], U8)
         w_scale = sb("w_scale", [P, 2, PASSES, M], U8)
-        picked = [[sb(f"picked{a}_{h}", [P, PACK, HALF], F32) for h in range(2)] for a in range(PASSES)]
+        picked = {}
+        for a in range(PASSES - 1):
+            for h in range(2):
+                picked[a, h, 0] = sb(f"picked{a}_{h}", [P, PACK, HALF], F32)
+        for h in range(2):
+            picked[2, h, 0] = sb(f"picked2_{h}_0", [P, 2, HALF], F32)
+        picked[2, 0, 2] = sb("picked2_0_2", [P, 2, HALF], F32)
+        gate = sb("gate", [P, 8], F32, "picked2_1_2")
         early = [sb(f"early{h}", [P, PASSES - 1, HALF, PACK], BF16) for h in range(2)]
         last_pass = [sb(f"last{h}", [P, 1, HALF, PACK], BF16) for h in range(2)]
         x_scale = [sb(f"x_scale{h}", [P, PASSES, HALF], U8) for h in range(2)]
@@ -65,7 +72,8 @@ def tile_list_hboth_none_kernel(
         nc.sync.dma_start(out=wgt_sb[1][:], in_=wgt[:, HALF:])
         for n in range(1, PASSES * PACK):
             load_plane(n // PACK, n % PACK)
-        nc.sync.dma_start(out=wgt_sb[2][:], in_=wgt[:, HALF:])
+        nc.sync.dma_start(out=gate[:], in_=wgt[:, :8])
+        picked[2, 1, 2] = sb("picked2_1_2", [P, 2, HALF], F32)
         nc.sync.dma_start(out=w4_sb[:].bitcast(I32), in_=w4_words.rearrange("a p n -> p a n").bitcast(I32))
         nc.sync.dma_start(out=r8_sb[:].bitcast(I32), in_=r8_words.rearrange("a p n i -> p a (n i)").bitcast(I32))
         nc.sync.dma_start(scatter_list[:], offs2)
@@ -82,13 +90,14 @@ def tile_list_hboth_none_kernel(
 
         def gather(a, i, h, weights, cols=slice(0, HALF)):
             offsets = list_part(gather_list, h * HALF + cols.start, cols.stop - cols.start)
-            nc.vector.tensor_tensor(picked[a][h][:, i, cols], planes[a][i][:].indirect(offsets), weights, MULT)
+            first = 2 if a == PASSES - 1 and i >= 2 else 0
+            nc.vector.tensor_tensor(picked[a, h, first][:, i - first, cols], planes[a][i][:].indirect(offsets), weights, MULT)
 
         def interleave(a, h, first, last, cols=slice(0, HALF)):
             grouped = early[h][:, a] if a < PASSES - 1 else last_pass[h][:, 0]
             nc.scalar.copy(
                 out=grouped[:, cols, first:last],
-                in_=picked[a][h][:, first:last, cols].rearrange("p i c -> p c i"),
+                in_=picked[a, h, first][:, :, cols].rearrange("p i c -> p c i"),
             )
 
         def quantize(h, first, last, tag=None, pieces=1):
@@ -105,20 +114,29 @@ def tile_list_hboth_none_kernel(
                     in_=grouped[:].rearrange("p a c i -> p (a c) i")[:, cols, :].rearrange("p c i -> p (c i)"),
                 )
 
-        def multiply(a, h, start, stop):
+        def product(w, a, h, q, start=False, stop=False):
+            cols = slice(q * N_MM, (q + 1) * N_MM)
+            nc.tensor.matmul_mx(
+                out=acc[h][q][:],
+                lhsT=r8_sb[:, a, :].bitcast(FP8X4) if w else w4_sb[:, a, :].bitcast(FP4X4),
+                lhsT_scale=w_scale[:, w, a, :],
+                rhs=codes[a, h][:, cols].bitcast(FP8X4),
+                rhs_scale=x_scale[h][:, a, cols],
+                start=start,
+                stop=stop,
+            )
+
+        def multiply_early(h):
+            for w in range(2):
+                for a in range(PASSES - 1):
+                    for q in range(2):
+                        product(w, a, h, q, start=(w == 0 and a == 0))
+
+        def multiply_last(h):
             for q in range(2):
-                cols = slice(q * N_MM, (q + 1) * N_MM)
-                rhs = codes[a, h][:, cols].bitcast(FP8X4)
-                nc.tensor.matmul_mx(
-                    out=acc[h][q][:], lhsT=w4_sb[:, a, :].bitcast(FP4X4), lhsT_scale=w_scale[:, 0, a, :],
-                    rhs=rhs, rhs_scale=x_scale[h][:, a, cols], start=start, stop=False,
-                )
-                nc.tensor.matmul_mx(
-                    out=acc[h][q][:], lhsT=r8_sb[:, a, :].bitcast(FP8X4), lhsT_scale=w_scale[:, 1, a, :],
-                    rhs=rhs, rhs_scale=x_scale[h][:, a, cols], start=False, stop=stop,
-                )
-                if stop:
-                    nc.scalar.copy(out=y_sb[h][:, cols], in_=acc[h][q][:])
+                product(0, PASSES - 1, h, q)
+                product(1, PASSES - 1, h, q, stop=True)
+                nc.scalar.copy(out=y_sb[h][:, q * N_MM : (q + 1) * N_MM], in_=acc[h][q][:])
 
         def scatter(h):
             nc.vector.tensor_tensor(
@@ -141,23 +159,21 @@ def tile_list_hboth_none_kernel(
         gather_plane(2, 1)
         for h in range(2):
             interleave(2, h, 0, 2)
-        quantize(0, 0, 2)
-        multiply(0, 0, True, False)
-        multiply(1, 0, False, False)
+        quantize(0, 0, 2, "picked1_1")
+        multiply_early(0)
         gather(2, 2, 0, wgt_sb[0][:])
         gather(2, 3, 0, wgt_sb[0][:])
         interleave(2, 0, 2, PACK)
         for cols in (slice(0, N_MM), slice(N_MM, HALF)):
-            gather(2, 2, 1, wgt_sb[2][:, cols], cols)
-            gather(2, 3, 1, wgt_sb[2][:, cols], cols)
+            gather(2, 2, 1, wgt_sb[1][:, cols], cols)
+            gather(2, 3, 1, wgt_sb[1][:, cols], cols)
             interleave(2, 1, 2, PACK, cols)
         quantize(0, 2, 3, pieces=2)
-        multiply(2, 0, False, True)
-        quantize(1, 0, 2, "picked2_0")
+        multiply_last(0)
+        quantize(1, 0, 2, "picked2_0_2")
         quantize(1, 2, 3)
-        multiply(0, 1, True, False)
-        multiply(1, 1, False, False)
-        multiply(2, 1, False, True)
+        multiply_early(1)
+        multiply_last(1)
         scatter(0)
         scatter(1)
         nc.sync.dma_start(out=out, in_=out_sb[:])

@@ -96,8 +96,8 @@ def tile_list_hboth_none_kernel(
         def interleave(a, h, first, last, cols=slice(0, HALF)):
             grouped = early[h][:, a] if a < PASSES - 1 else last_pass[h][:, 0]
             nc.scalar.copy(
-                out=grouped[:, cols, first:last],
-                in_=picked[a, h, first][:, :, cols].rearrange("p i c -> p c i"),
+                out=grouped[:, cols, first:last].rearrange("p (c j) i -> p c i j", j=4),
+                in_=picked[a, h, first][:, :, cols].rearrange("p i (c j) -> p c i j", j=4),
             )
 
         def quantize(h, first, last, tag=None, pieces=1):

@@ -37,23 +37,18 @@ def tile_list_hboth_none_kernel(
 
         gather_list = keep.tile([P, S // LIST_ROWS], U16, name="gather_list")
         scatter_list = keep.tile([P, S // LIST_ROWS], U16, name="scatter_list")
-        wgt_sb = [sb(f"wgt{h}", [P, HALF], F32) for h in range(2)]
+        wgt_sb = sb("wgt", [P, 3 * HALF], F32)
         wgo_sb = sb("wgo", [P, S], F32)
         planes = [[sb(f"plane{a}_{i}", [P, T], F32) for i in range(PACK)] for a in range(PASSES)]
         w4_sb = sb("w4", [P, PASSES, 2 * M], U8)
         r8_sb = sb("r8", [P, PASSES, PACK * M], U8)
         w_scale = sb("w_scale", [P, 2, PASSES, M], U8)
-        picked = {}
-        for a in range(PASSES - 1):
-            for h in range(2):
-                picked[a, h, 0] = sb(f"picked{a}_{h}", [P, PACK, HALF], F32)
-        for h in range(2):
-            picked[2, h, 0] = sb(f"picked2_{h}_0", [P, 2, HALF], F32)
-        picked[2, 0, 2] = sb("picked2_0_2", [P, 2, HALF], F32)
-        gate = sb("gate", [P, 8], F32, "picked2_1_2")
+        picked = [sb(f"picked{a}", [P, PACK if a < 2 else 2, S], F32) for a in range(PASSES)]
+        tail_a = sb("tail_a", [P, 2, HALF], F32)[:]
+        tail_b = wgt_sb[:].rearrange("p (i c) -> p i c", c=HALF)[:, 0:3:2, :]
         early = [sb(f"early{h}", [P, PASSES - 1, HALF, PACK], BF16) for h in range(2)]
         last_pass = [sb(f"last{h}", [P, 1, HALF, PACK], BF16) for h in range(2)]
-        x_scale = [sb(f"x_scale{h}", [P, PASSES, HALF], U8) for h in range(2)]
+        x_scale = {}
         codes = {}
         y_sb = [sb(f"y{h}", [P, HALF], F32) for h in range(2)]
         out_sb = sb("out_sb", [P, T], F32)
@@ -68,49 +63,49 @@ def tile_list_hboth_none_kernel(
 
         load_plane(0, 0)
         nc.sync.dma_start(gather_list[:], offs)
-        nc.sync.dma_start(out=wgt_sb[0][:], in_=wgt[:, :HALF])
-        nc.sync.dma_start(out=wgt_sb[1][:], in_=wgt[:, HALF:])
+        nc.sync.dma_start(out=wgt_sb[:, :HALF], in_=wgt[:, :HALF])
+        nc.sync.dma_start(out=wgt_sb[:, HALF:S], in_=wgt[:, HALF:])
         for n in range(1, PASSES * PACK):
             load_plane(n // PACK, n % PACK)
-        nc.sync.dma_start(out=gate[:], in_=wgt[:, :8])
-        picked[2, 1, 2] = sb("picked2_1_2", [P, 2, HALF], F32)
         nc.sync.dma_start(out=w4_sb[:].bitcast(I32), in_=w4_words.rearrange("a p n -> p a n").bitcast(I32))
         nc.sync.dma_start(out=r8_sb[:].bitcast(I32), in_=r8_words.rearrange("a p n i -> p a (n i)").bitcast(I32))
-        nc.sync.dma_start(scatter_list[:], offs2)
-        nc.sync.dma_start(out=wgo_sb[:], in_=wgo)
         for w, scales in enumerate((w4_scales, r8_scales)):
             for quad in range(4):
                 nc.gpsimd.dma_start(
                     out=w_scale[32 * quad : 32 * quad + 4, w].bitcast(I32),
                     in_=scales[:, 4 * quad : 4 * quad + 4, :].rearrange("a r n -> r a n").bitcast(I32),
                 )
+        nc.sync.dma_start(scatter_list[:], offs2)
+        nc.sync.dma_start(out=wgo_sb[:], in_=wgo)
 
         def list_part(lst, first, count):
             return lst[:, first // LIST_ROWS : (first + count) // LIST_ROWS]
 
-        def gather(a, i, h, weights, cols=slice(0, HALF)):
-            offsets = list_part(gather_list, h * HALF + cols.start, cols.stop - cols.start)
-            first = 2 if a == PASSES - 1 and i >= 2 else 0
-            nc.vector.tensor_tensor(picked[a, h, first][:, i - first, cols], planes[a][i][:].indirect(offsets), weights, MULT)
-
-        def interleave(a, h, first, last, cols=slice(0, HALF)):
-            grouped = early[h][:, a] if a < PASSES - 1 else last_pass[h][:, 0]
-            nc.scalar.copy(
-                out=grouped[:, cols, first:last].rearrange("p (c j) i -> p c i j", j=4),
-                in_=picked[a, h, first][:, :, cols].rearrange("p i (c j) -> p c i j", j=4),
+        def gather(dst, a, i, first, count):
+            nc.vector.tensor_tensor(
+                dst, planes[a][i][:].indirect(list_part(gather_list, first, count)), wgt_sb[:, first : first + count], MULT
             )
 
+        def gather_plane(a, i, pieces=1):
+            for first in range(0, S, S // pieces):
+                gather(picked[a][:, i, first : first + S // pieces], a, i, first, S // pieces)
+
+        def interleave(dst, src):
+            nc.scalar.copy(out=dst.rearrange("p (c j) i -> p c i j", j=4), in_=src.rearrange("p i (c j) -> p c i j", j=4))
+
         def quantize(h, first, last, tag=None, pieces=1):
-            words = sb(f"codes{h}_{first}", [P, last - first, HALF], U32, tag)
+            words = sb(f"codes{h}_{first}", [P, last - first, HALF], U32, tag)[:]
+            scales = sb(f"x_scale{h}_{first}", [P, last - first, HALF], U8)[:]
             for a in range(first, last):
                 codes[a, h] = words[:, a - first, :]
+                x_scale[a, h] = scales[:, a - first, :]
             grouped = early[h] if first == 0 else last_pass[h]
             width = (last - first) * HALF // pieces
             for c0 in range(0, (last - first) * HALF, width):
                 cols = slice(c0, c0 + width)
                 nc.vector.quantize_mx(
-                    out=words[:].rearrange("p a c -> p (a c)")[:, cols].bitcast(FP8X4),
-                    scales=x_scale[h][:, first:last, :].rearrange("p a c -> p (a c)")[:, cols],
+                    out=words.rearrange("p a c -> p (a c)")[:, cols].bitcast(FP8X4),
+                    scales=scales.rearrange("p a c -> p (a c)")[:, cols],
                     in_=grouped[:].rearrange("p a c i -> p (a c) i")[:, cols, :].rearrange("p c i -> p (c i)"),
                 )
 
@@ -121,16 +116,16 @@ def tile_list_hboth_none_kernel(
                 lhsT=r8_sb[:, a, :].bitcast(FP8X4) if w else w4_sb[:, a, :].bitcast(FP4X4),
                 lhsT_scale=w_scale[:, w, a, :],
                 rhs=codes[a, h][:, cols].bitcast(FP8X4),
-                rhs_scale=x_scale[h][:, a, cols],
+                rhs_scale=x_scale[a, h][:, cols],
                 start=start,
                 stop=stop,
             )
 
         def multiply_early(h):
-            for w in range(2):
+            for w in (1, 0):
                 for a in range(PASSES - 1):
                     for q in range(2):
-                        product(w, a, h, q, start=(w == 0 and a == 0))
+                        product(w, a, h, q, start=(w == 1 and a == 0))
 
         def multiply_last(h):
             for q in range(2):
@@ -138,42 +133,35 @@ def tile_list_hboth_none_kernel(
                 product(1, PASSES - 1, h, q, stop=True)
                 nc.scalar.copy(out=y_sb[h][:, q * N_MM : (q + 1) * N_MM], in_=acc[h][q][:])
 
-        def scatter(h):
+        def scatter(values, first, count):
             nc.vector.tensor_tensor(
-                out_sb[:].indirect(list_part(scatter_list, h * HALF, HALF)),
-                y_sb[h][:],
-                wgo_sb[:, h * HALF : (h + 1) * HALF],
-                MULT,
+                out_sb[:].indirect(list_part(scatter_list, first, count)), values, wgo_sb[:, first : first + count], MULT
             )
 
-        def gather_plane(a, i):
-            for h in range(2):
-                gather(a, i, h, wgt_sb[h][:])
-
+        halves = [slice(0, HALF), slice(HALF, S)]
         for a in range(2):
             for i in range(PACK):
-                gather_plane(a, i)
+                gather_plane(a, i, 2 if (a, i) in ((0, 0), (1, 3)) else 1)
             for h in range(2):
-                interleave(a, h, 0, PACK)
-        gather_plane(2, 0)
-        gather_plane(2, 1)
-        for h in range(2):
-            interleave(2, h, 0, 2)
-        quantize(0, 0, 2, "picked1_1")
+                interleave(early[h][:, a], picked[a][:, :, halves[h]])
+        quantize(0, 0, 2)
         multiply_early(0)
-        gather(2, 2, 0, wgt_sb[0][:])
-        gather(2, 3, 0, wgt_sb[0][:])
-        interleave(2, 0, 2, PACK)
-        for cols in (slice(0, N_MM), slice(N_MM, HALF)):
-            gather(2, 2, 1, wgt_sb[1][:, cols], cols)
-            gather(2, 3, 1, wgt_sb[1][:, cols], cols)
-            interleave(2, 1, 2, PACK, cols)
+        gather_plane(2, 0)
+        gather_plane(2, 1, 2)
+        for h in range(2):
+            interleave(last_pass[h][:, 0, :, 0:2], picked[2][:, :, halves[h]])
+        gather(tail_a[:, 0, :], 2, 2, 0, HALF)
+        gather(tail_a[:, 1, :], 2, 3, 0, HALF)
+        interleave(last_pass[0][:, 0, :, 2:4], tail_a)
+        gather(tail_b[:, 1, :], 2, 3, HALF, HALF)
+        gather(tail_b[:, 0, :], 2, 2, HALF, HALF)
+        interleave(last_pass[1][:, 0, :, 2:4], tail_b)
         quantize(0, 2, 3, pieces=2)
         multiply_last(0)
-        quantize(1, 0, 2, "picked2_0_2")
+        quantize(1, 0, 2, "tail_a")
         quantize(1, 2, 3)
         multiply_early(1)
         multiply_last(1)
-        scatter(0)
-        scatter(1)
+        scatter(y_sb[0][:], 0, HALF)
+        scatter(y_sb[1][:], HALF, HALF)
         nc.sync.dma_start(out=out, in_=out_sb[:])

@@ -42,7 +42,7 @@ def tile_list_hboth_none_kernel(
         planes = [[sb(f"plane{a}_{i}", [P, T], F32) for i in range(PACK)] for a in range(PASSES)]
         w4_sb = sb("w4", [P, PASSES, 2 * M], U8)
         r8_sb = sb("r8", [P, PASSES, PACK * M], U8)
-        w_scale = sb("w_scale", [P, 2, PASSES, M], U8)
+        w_scale = {1: sb("r8_scale", [P, PASSES, M], U8)}
         picked = [sb(f"picked{a}", [P, PACK if a < 2 else 2, S], F32) for a in range(PASSES)]
         tail_a = sb("tail_a", [P, 2, HALF], F32)[:]
         tail_b = wgt_sb[:].rearrange("p (i c) -> p i c", c=HALF)[:, 0:3:2, :]
@@ -54,12 +54,19 @@ def tile_list_hboth_none_kernel(
         out_sb = sb("out_sb", [P, T], F32)
         acc = [[psum.tile([P, N_MM], F32, name=f"acc{h}_{q}") for q in range(2)] for h in range(2)]
 
-        nc.vector.memset(w_scale[:].rearrange("p w a n -> p (w a n)").bitcast(I32), 0)
+        nc.vector.memset(w_scale[1][:].rearrange("p a n -> p (a n)").bitcast(I32), 0)
         nc.vector.memset(out_sb[:], 0.0)
 
         def load_plane(a, i):
             rows = xT[a * K_PASS : (a + 1) * K_PASS, :].rearrange("(p i) t -> p i t", i=PACK)
             nc.sync.dma_start(out=planes[a][i][:], in_=rows[:, i, :])
+
+        def load_scales(queue, tile, scales):
+            for quad in range(4):
+                queue.dma_start(
+                    out=tile[32 * quad : 32 * quad + 4].bitcast(I32),
+                    in_=scales[:, 4 * quad : 4 * quad + 4, :].rearrange("a r n -> r a n").bitcast(I32),
+                )
 
         load_plane(0, 0)
         nc.sync.dma_start(gather_list[:], offs)
@@ -69,12 +76,7 @@ def tile_list_hboth_none_kernel(
             load_plane(n // PACK, n % PACK)
         nc.sync.dma_start(out=w4_sb[:].bitcast(I32), in_=w4_words.rearrange("a p n -> p a n").bitcast(I32))
         nc.sync.dma_start(out=r8_sb[:].bitcast(I32), in_=r8_words.rearrange("a p n i -> p a (n i)").bitcast(I32))
-        for w, scales in enumerate((w4_scales, r8_scales)):
-            for quad in range(4):
-                nc.gpsimd.dma_start(
-                    out=w_scale[32 * quad : 32 * quad + 4, w].bitcast(I32),
-                    in_=scales[:, 4 * quad : 4 * quad + 4, :].rearrange("a r n -> r a n").bitcast(I32),
-                )
+        load_scales(nc.sync, w_scale[1], r8_scales)
         nc.sync.dma_start(scatter_list[:], offs2)
         nc.sync.dma_start(out=wgo_sb[:], in_=wgo)
 
@@ -114,7 +116,7 @@ def tile_list_hboth_none_kernel(
             nc.tensor.matmul_mx(
                 out=acc[h][q][:],
                 lhsT=r8_sb[:, a, :].bitcast(FP8X4) if w else w4_sb[:, a, :].bitcast(FP4X4),
-                lhsT_scale=w_scale[:, w, a, :],
+                lhsT_scale=w_scale[w][:, a, :],
                 rhs=codes[a, h][:, cols].bitcast(FP8X4),
                 rhs_scale=x_scale[a, h][:, cols],
                 start=start,
@@ -144,6 +146,9 @@ def tile_list_hboth_none_kernel(
                 gather_plane(a, i, 2 if (a, i) in ((0, 0), (1, 3)) else 1)
             for h in range(2):
                 interleave(early[h][:, a], picked[a][:, :, halves[h]])
+        w_scale[0] = sb("w4_scale", [P, PASSES, M], U8, "plane0_1")
+        nc.gpsimd.memset(w_scale[0][:].rearrange("p a n -> p (a n)").bitcast(I32), 0)
+        load_scales(nc.gpsimd, w_scale[0], w4_scales)
         quantize(0, 0, 2)
         multiply_early(0)
         gather_plane(2, 0)

@@ -56,6 +56,9 @@ def tile_list_hboth_none_kernel(
 
         nc.vector.memset(w_scale[1][:].rearrange("p a n -> p (a n)").bitcast(I32), 0)
         nc.vector.memset(out_sb[:], 0.0)
+        wgt_rows = sb("wgt_rows", [P, 32], F32)
+        wgt_turned = sb("wgt_turned", [P, 32], F32)
+        wgt_wide = sb("wgt_wide", [P, S], F32)
 
         def load_plane(a, i):
             rows = xT[a * K_PASS : (a + 1) * K_PASS, :].rearrange("(p i) t -> p i t", i=PACK)
@@ -68,10 +71,18 @@ def tile_list_hboth_none_kernel(
                     in_=scales[:, 4 * quad : 4 * quad + 4, :].rearrange("a r n -> r a n").bitcast(I32),
                 )
 
+        nc.sync.dma_start(out=wgt_rows[:], in_=wgt[0:P:LIST_ROWS, :].rearrange("g (b s) -> g b s", s=32))
         load_plane(0, 0)
         nc.sync.dma_start(gather_list[:], offs)
-        nc.sync.dma_start(out=wgt_sb[:, :HALF], in_=wgt[:, :HALF])
-        nc.sync.dma_start(out=wgt_sb[:, HALF:S], in_=wgt[:, HALF:])
+        nc.vector.transpose(wgt_turned[:], wgt_rows[:])
+        wide = wgt_wide[:].rearrange("p (b h r) -> p b h r", h=2, r=LIST_ROWS)
+        turned = wgt_turned[:].rearrange("p (h b) -> p b h", h=2)
+        for h in range(2):
+            nc.vector.tensor_copy(
+                out=wide[:, 8 * h : 8 * h + 8], in_=turned[:, 8 * h : 8 * h + 8].unsqueeze(3).to_broadcast([P, 8, 2, LIST_ROWS])
+            )
+        for h in range(2):
+            nc.vector.transpose(wgt_sb[:, h * HALF : (h + 1) * HALF], wgt_wide[:, h * HALF : (h + 1) * HALF])
         for n in range(1, PASSES * PACK):
             load_plane(n // PACK, n % PACK)
         nc.sync.dma_start(out=w4_sb[:].bitcast(I32), in_=w4_words.rearrange("a p n -> p a n").bitcast(I32))

@@ -58,7 +58,7 @@ def tile_list_hboth_none_kernel(
         nc.vector.memset(out_sb[:], 0.0)
         wgt_rows = sb("wgt_rows", [P, 32], F32)
         wgt_turned = sb("wgt_turned", [P, 32], F32)
-        wgt_wide = sb("wgt_wide", [P, S], F32)
+        wgt_wide = sb("wgt_wide", [P, HALF], F32)
 
         def load_plane(a, i):
             rows = xT[a * K_PASS : (a + 1) * K_PASS, :].rearrange("(p i) t -> p i t", i=PACK)
@@ -71,18 +71,19 @@ def tile_list_hboth_none_kernel(
                     in_=scales[:, 4 * quad : 4 * quad + 4, :].rearrange("a r n -> r a n").bitcast(I32),
                 )
 
-        nc.sync.dma_start(out=wgt_rows[:], in_=wgt[0:P:LIST_ROWS, :].rearrange("g (b s) -> g b s", s=32))
+        nc.sync.dma_start(out=wgt_rows[:], in_=wgt[0:P:8, :HALF].rearrange("e (b s) -> e b s", s=32))
         load_plane(0, 0)
         nc.sync.dma_start(gather_list[:], offs)
+        nc.sync.dma_start(out=wgt_sb[:, HALF:S], in_=wgt[:, HALF:])
         nc.vector.transpose(wgt_turned[:], wgt_rows[:])
-        wide = wgt_wide[:].rearrange("p (b h r) -> p b h r", h=2, r=LIST_ROWS)
-        turned = wgt_turned[:].rearrange("p (h b) -> p b h", h=2)
+        wide = wgt_wide[:].rearrange("p (b e r) -> p b e r", e=4, r=8)
+        turned = wgt_turned[:].rearrange("p (e b) -> p b e", e=4)
         for h in range(2):
             nc.vector.tensor_copy(
-                out=wide[:, 8 * h : 8 * h + 8], in_=turned[:, 8 * h : 8 * h + 8].unsqueeze(3).to_broadcast([P, 8, 2, LIST_ROWS])
+                out=wide[:, 4 * h : 4 * h + 4], in_=turned[:, 4 * h : 4 * h + 4].unsqueeze(3).to_broadcast([P, 4, 4, 8])
             )
         for h in range(2):
-            nc.vector.transpose(wgt_sb[:, h * HALF : (h + 1) * HALF], wgt_wide[:, h * HALF : (h + 1) * HALF])
+            nc.vector.transpose(wgt_sb[:, h * N_MM : (h + 1) * N_MM], wgt_wide[:, h * N_MM : (h + 1) * N_MM])
         for n in range(1, PASSES * PACK):
             load_plane(n // PACK, n % PACK)
         nc.sync.dma_start(out=w4_sb[:].bitcast(I32), in_=w4_words.rearrange("a p n -> p a n").bitcast(I32))
@@ -154,16 +155,20 @@ def tile_list_hboth_none_kernel(
         halves = [slice(0, HALF), slice(HALF, S)]
         for a in range(2):
             for i in range(PACK):
-                gather_plane(a, i, 2 if (a, i) in ((0, 0), (1, 3)) else 1)
-            for h in range(2):
-                interleave(early[h][:, a], picked[a][:, :, halves[h]])
+                gather_plane(a, i, 2 if (a, i) == (0, 0) else 1)
+            if a == 0:
+                interleave(early[0][:, a], picked[a][:, :, halves[0]])
+            else:
+                for i in (0, 2):
+                    interleave(early[0][:, a, :, i : i + 2], picked[a][:, i : i + 2, halves[0]])
+            interleave(early[1][:, a], picked[a][:, :, halves[1]])
         w_scale[0] = sb("w4_scale", [P, PASSES, M], U8, "plane0_1")
         nc.gpsimd.memset(w_scale[0][:].rearrange("p a n -> p (a n)").bitcast(I32), 0)
         load_scales(nc.gpsimd, w_scale[0], w4_scales)
-        quantize(0, 0, 2)
-        multiply_early(0)
         gather_plane(2, 0)
-        gather_plane(2, 1, 2)
+        gather_plane(2, 1)
+        quantize(0, 0, 2, "picked1")
+        multiply_early(0)
         for h in range(2):
             interleave(last_pass[h][:, 0, :, 0:2], picked[2][:, :, halves[h]])
         gather(tail_a[:, 0, :], 2, 2, 0, HALF)

@@ -175,8 +175,10 @@ def tile_list_hboth_none_kernel(
         gather(tail_a[:, 1, :], 2, 3, 0, HALF)
         interleave(last_pass[0][:, 0, :, 2:4], tail_a)
         gather(tail_b[:, 1, :], 2, 3, HALF, HALF)
-        gather(tail_b[:, 0, :], 2, 2, HALF, HALF)
-        interleave(last_pass[1][:, 0, :, 2:4], tail_b)
+        for q in range(2):
+            cols = slice(q * N_MM, (q + 1) * N_MM)
+            gather(tail_b[:, 0, cols], 2, 2, HALF + q * N_MM, N_MM)
+            interleave(last_pass[1][:, 0, cols, 2:4], tail_b[:, :, cols])
         quantize(0, 2, 3, pieces=2)
         multiply_last(0)
         quantize(1, 0, 2, "tail_a")

@@ -19,8 +19,9 @@ P = 128
 PACK = 4
 K_PASS = P * PACK
 PASSES = K // K_PASS
+LAST = PASSES - 1
 HALF = S // 2
-N_MM = 128
+QUARTER = S // 4
 LIST_ROWS = 16
 
 
@@ -37,28 +38,26 @@ def tile_list_hboth_none_kernel(
 
         gather_list = keep.tile([P, S // LIST_ROWS], U16, name="gather_list")
         scatter_list = keep.tile([P, S // LIST_ROWS], U16, name="scatter_list")
-        wgt_sb = sb("wgt", [P, 3 * HALF], F32)
-        wgo_sb = sb("wgo", [P, S], F32)
         planes = [[sb(f"plane{a}_{i}", [P, T], F32) for i in range(PACK)] for a in range(PASSES)]
+        picked = [sb(f"picked{a}", [P, PACK * S], F32)[:].rearrange("p (i j) -> p i j", j=S) for a in range(PASSES)]
+        wgt_sb = picked[LAST].rearrange("p i j -> p (i j)")[:, 2 * S + HALF : 3 * S + HALF]
+        wgo_sb = sb("wgo", [P, S], F32)
         w4_sb = sb("w4", [P, PASSES, 2 * M], U8)
         r8_sb = sb("r8", [P, PASSES, PACK * M], U8)
-        w_scale = {1: sb("r8_scale", [P, PASSES, M], U8)}
-        picked = [sb(f"picked{a}", [P, PACK if a < 2 else 2, S], F32) for a in range(PASSES)]
-        tail_a = sb("tail_a", [P, 2, HALF], F32)[:]
-        tail_b = wgt_sb[:].rearrange("p (i c) -> p i c", c=HALF)[:, 0:3:2, :]
-        early = [sb(f"early{h}", [P, PASSES - 1, HALF, PACK], BF16) for h in range(2)]
-        last_pass = [sb(f"last{h}", [P, 1, HALF, PACK], BF16) for h in range(2)]
-        x_scale = {}
-        codes = {}
-        y_sb = [sb(f"y{h}", [P, HALF], F32) for h in range(2)]
+        r8_scale = sb("r8_scale", [P, PASSES, M], U8)
+        tail_a = sb("tail_a", [P, 2, HALF], F32)
+        early_first = sb("early_first", [P, LAST, QUARTER, PACK], BF16)
+        early_rest = sb("early_rest", [P, LAST, S - QUARTER, PACK], BF16)
+        last_a = sb("last_a", [P, HALF, PACK], BF16)
         out_sb = sb("out_sb", [P, T], F32)
-        acc = [[psum.tile([P, N_MM], F32, name=f"acc{h}_{q}") for q in range(2)] for h in range(2)]
-
-        nc.vector.memset(w_scale[1][:].rearrange("p a n -> p (a n)").bitcast(I32), 0)
-        nc.vector.memset(out_sb[:], 0.0)
+        y_sb = [sb("y0", [P, QUARTER], F32), sb("y1", [P, QUARTER], F32), sb("y23", [P, HALF], F32)]
+        acc = [psum.tile([P, QUARTER], F32, name=f"acc{q}") for q in range(4)]
         wgt_rows = sb("wgt_rows", [P, 32], F32)
         wgt_turned = sb("wgt_turned", [P, 32], F32)
         wgt_wide = sb("wgt_wide", [P, HALF], F32)
+
+        nc.vector.memset(r8_scale[:].rearrange("p a n -> p (a n)").bitcast(I32), 0)
+        nc.vector.memset(out_sb[:], 0.0)
 
         def load_plane(a, i):
             rows = xT[a * K_PASS : (a + 1) * K_PASS, :].rearrange("(p i) t -> p i t", i=PACK)
@@ -74,21 +73,21 @@ def tile_list_hboth_none_kernel(
         nc.sync.dma_start(out=wgt_rows[:], in_=wgt[0:P:8, :HALF].rearrange("e (b s) -> e b s", s=32))
         load_plane(0, 0)
         nc.sync.dma_start(gather_list[:], offs)
-        nc.sync.dma_start(out=wgt_sb[:, HALF:S], in_=wgt[:, HALF:])
+        nc.sync.dma_start(out=wgt_sb[:, HALF:], in_=wgt[:, HALF:])
         nc.vector.transpose(wgt_turned[:], wgt_rows[:])
         wide = wgt_wide[:].rearrange("p (b e r) -> p b e r", e=4, r=8)
         turned = wgt_turned[:].rearrange("p (e b) -> p b e", e=4)
-        for h in range(2):
+        for q in range(2):
             nc.vector.tensor_copy(
-                out=wide[:, 4 * h : 4 * h + 4], in_=turned[:, 4 * h : 4 * h + 4].unsqueeze(3).to_broadcast([P, 4, 4, 8])
+                out=wide[:, 4 * q : 4 * q + 4], in_=turned[:, 4 * q : 4 * q + 4].unsqueeze(3).to_broadcast([P, 4, 4, 8])
             )
-        for h in range(2):
-            nc.vector.transpose(wgt_sb[:, h * N_MM : (h + 1) * N_MM], wgt_wide[:, h * N_MM : (h + 1) * N_MM])
+        for q in range(2):
+            nc.vector.transpose(wgt_sb[:, q * QUARTER : (q + 1) * QUARTER], wgt_wide[:, q * QUARTER : (q + 1) * QUARTER])
         for n in range(1, PASSES * PACK):
             load_plane(n // PACK, n % PACK)
         nc.sync.dma_start(out=w4_sb[:].bitcast(I32), in_=w4_words.rearrange("a p n -> p a n").bitcast(I32))
         nc.sync.dma_start(out=r8_sb[:].bitcast(I32), in_=r8_words.rearrange("a p n i -> p a (n i)").bitcast(I32))
-        load_scales(nc.sync, w_scale[1], r8_scales)
+        load_scales(nc.sync, r8_scale, r8_scales)
         nc.sync.dma_start(scatter_list[:], offs2)
         nc.sync.dma_start(out=wgo_sb[:], in_=wgo)
 
@@ -100,91 +99,99 @@ def tile_list_hboth_none_kernel(
                 dst, planes[a][i][:].indirect(list_part(gather_list, first, count)), wgt_sb[:, first : first + count], MULT
             )
 
-        def gather_plane(a, i, pieces=1):
-            for first in range(0, S, S // pieces):
-                gather(picked[a][:, i, first : first + S // pieces], a, i, first, S // pieces)
-
         def interleave(dst, src):
             nc.scalar.copy(out=dst.rearrange("p (c j) i -> p c i j", j=4), in_=src.rearrange("p i (c j) -> p c i j", j=4))
 
-        def quantize(h, first, last, tag=None, pieces=1):
-            words = sb(f"codes{h}_{first}", [P, last - first, HALF], U32, tag)[:]
-            scales = sb(f"x_scale{h}_{first}", [P, last - first, HALF], U8)[:]
-            for a in range(first, last):
-                codes[a, h] = words[:, a - first, :]
-                x_scale[a, h] = scales[:, a - first, :]
-            grouped = early[h] if first == 0 else last_pass[h]
-            width = (last - first) * HALF // pieces
-            for c0 in range(0, (last - first) * HALF, width):
-                cols = slice(c0, c0 + width)
-                nc.vector.quantize_mx(
-                    out=words.rearrange("p a c -> p (a c)")[:, cols].bitcast(FP8X4),
-                    scales=scales.rearrange("p a c -> p (a c)")[:, cols],
-                    in_=grouped[:].rearrange("p a c i -> p (a c) i")[:, cols, :].rearrange("p c i -> p (c i)"),
-                )
+        operand = {}
 
-        def product(w, a, h, q, start=False, stop=False):
-            cols = slice(q * N_MM, (q + 1) * N_MM)
-            nc.tensor.matmul_mx(
-                out=acc[h][q][:],
-                lhsT=r8_sb[:, a, :].bitcast(FP8X4) if w else w4_sb[:, a, :].bitcast(FP4X4),
-                lhsT_scale=w_scale[w][:, a, :],
-                rhs=codes[a, h][:, cols].bitcast(FP8X4),
-                rhs_scale=x_scale[a, h][:, cols],
-                start=start,
-                stop=stop,
+        def mx_tiles(name, width, tag=None):
+            return sb(f"codes_{name}", [P, width], U32, tag), sb(f"scales_{name}", [P, width], U8)
+
+        def quantize(tiles, first, grouped, keys):
+            cols = slice(first, first + len(keys) * QUARTER)
+            nc.vector.quantize_mx(
+                out=tiles[0][:, cols].bitcast(FP8X4), scales=tiles[1][:, cols], in_=grouped.rearrange("p c i -> p (c i)")
             )
+            for n, key in enumerate(keys):
+                part = slice(first + n * QUARTER, first + (n + 1) * QUARTER)
+                operand[key] = (tiles[0][:, part], tiles[1][:, part])
 
-        def multiply_early(h):
-            for w in (1, 0):
-                for a in range(PASSES - 1):
-                    for q in range(2):
-                        product(w, a, h, q, start=(w == 1 and a == 0))
-
-        def multiply_last(h):
-            for q in range(2):
-                product(0, PASSES - 1, h, q)
-                product(1, PASSES - 1, h, q, stop=True)
-                nc.scalar.copy(out=y_sb[h][:, q * N_MM : (q + 1) * N_MM], in_=acc[h][q][:])
+        def products(q, a, start=False, stop=False):
+            codes, scales = operand[a, q]
+            for n, (lhs, lhs_scale) in enumerate(
+                ((r8_sb[:, a, :].bitcast(FP8X4), r8_scale), (w4_sb[:, a, :].bitcast(FP4X4), w4_scale))
+            ):
+                nc.tensor.matmul_mx(
+                    out=acc[q][:],
+                    lhsT=lhs,
+                    lhsT_scale=lhs_scale[:, a, :],
+                    rhs=codes.bitcast(FP8X4),
+                    rhs_scale=scales,
+                    start=start and n == 0,
+                    stop=stop and n == 1,
+                )
 
         def scatter(values, first, count):
             nc.vector.tensor_tensor(
                 out_sb[:].indirect(list_part(scatter_list, first, count)), values, wgo_sb[:, first : first + count], MULT
             )
 
-        halves = [slice(0, HALF), slice(HALF, S)]
-        for a in range(2):
+        quarter = [slice(q * QUARTER, (q + 1) * QUARTER) for q in range(4)]
+        for a in range(LAST):
             for i in range(PACK):
-                gather_plane(a, i, 2 if (a, i) == (0, 0) else 1)
-            if a == 0:
-                interleave(early[0][:, a], picked[a][:, :, halves[0]])
-            else:
-                for i in (0, 2):
-                    interleave(early[0][:, a, :, i : i + 2], picked[a][:, i : i + 2, halves[0]])
-            interleave(early[1][:, a], picked[a][:, :, halves[1]])
-        w_scale[0] = sb("w4_scale", [P, PASSES, M], U8, "plane0_1")
-        nc.gpsimd.memset(w_scale[0][:].rearrange("p a n -> p (a n)").bitcast(I32), 0)
-        load_scales(nc.gpsimd, w_scale[0], w4_scales)
-        gather_plane(2, 0)
-        gather_plane(2, 1)
-        quantize(0, 0, 2, "picked1")
-        multiply_early(0)
-        for h in range(2):
-            interleave(last_pass[h][:, 0, :, 0:2], picked[2][:, :, halves[h]])
-        gather(tail_a[:, 0, :], 2, 2, 0, HALF)
-        gather(tail_a[:, 1, :], 2, 3, 0, HALF)
-        interleave(last_pass[0][:, 0, :, 2:4], tail_a)
-        gather(tail_b[:, 1, :], 2, 3, HALF, HALF)
+                if (a, i) == (0, 0):
+                    gather(picked[a][:, i, :HALF], a, i, 0, HALF)
+                    gather(picked[a][:, i, HALF:], a, i, HALF, HALF)
+                else:
+                    gather(picked[a][:, i, :], a, i, 0, S)
+            interleave(early_first[:, a], picked[a][:, :, :QUARTER])
+            interleave(early_rest[:, a], picked[a][:, :, QUARTER:])
+        w4_scale = sb("w4_scale", [P, PASSES, M], U8, "plane0_1")
+        nc.gpsimd.memset(w4_scale[:].rearrange("p a n -> p (a n)").bitcast(I32), 0)
+        load_scales(nc.gpsimd, w4_scale, w4_scales)
+
+        gather(picked[LAST][:, 0, :], LAST, 0, 0, S)
+        quantize(
+            mx_tiles("early_first", LAST * QUARTER), 0, early_first[:].rearrange("p a c i -> p (a c) i"), [(0, 0), (1, 0)]
+        )
+        products(0, 0, start=True)
+        products(0, 1)
+        gather(picked[LAST][:, 1, :], LAST, 1, 0, S)
+        interleave(last_a[:, :, 0:2], picked[LAST][:, 0:2, :HALF])
+        gather(tail_a[:, 0, :], LAST, 2, 0, HALF)
+        gather(tail_a[:, 1, :], LAST, 3, 0, HALF)
         for q in range(2):
-            cols = slice(q * N_MM, (q + 1) * N_MM)
-            gather(tail_b[:, 0, cols], 2, 2, HALF + q * N_MM, N_MM)
-            interleave(last_pass[1][:, 0, cols, 2:4], tail_b[:, :, cols])
-        quantize(0, 2, 3, pieces=2)
-        multiply_last(0)
-        quantize(1, 0, 2, "tail_a")
-        quantize(1, 2, 3)
-        multiply_early(1)
-        multiply_last(1)
-        scatter(y_sb[0][:], 0, HALF)
-        scatter(y_sb[1][:], HALF, HALF)
+            interleave(last_a[:, quarter[q], 2:4], tail_a[:, :, quarter[q]])
+        gather(picked[LAST][:, 3, HALF:], LAST, 3, HALF, HALF)
+        gather(picked[LAST][:, 2, HALF:], LAST, 2, HALF, HALF)
+
+        first_tiles = mx_tiles("last0", QUARTER)
+        quantize(first_tiles, 0, last_a[:, quarter[0], :], [(LAST, 0)])
+        quantize(mx_tiles("last1", QUARTER), 0, last_a[:, quarter[1], :], [(LAST, 1)])
+        products(0, LAST, stop=True)
+        nc.scalar.copy(out=y_sb[0][:], in_=acc[0][:])
+        products(1, LAST, start=True)
+        rest_tiles = mx_tiles("early_rest", LAST * (S - QUARTER), "tail_a")
+        for a in range(LAST):
+            quantize(rest_tiles, a * (S - QUARTER), early_rest[:, a], [(a, 1), (a, 2), (a, 3)])
+        products(1, 0)
+        products(1, 1, stop=True)
+        nc.scalar.copy(out=y_sb[1][:], in_=acc[1][:])
+        products(2, 0, start=True)
+        products(2, 1)
+        last_q2 = sb("last_q2", [P, QUARTER, PACK], BF16)
+        interleave(last_q2[:], picked[LAST][:, :, quarter[2]])
+        quantize(mx_tiles("last2", QUARTER), 0, last_q2[:], [(LAST, 2)])
+        products(2, LAST, stop=True)
+        products(3, 1, start=True)
+        products(3, 0)
+        scatter(y_sb[0][:], 0, QUARTER)
+        last_q3 = sb("last_q3", [P, QUARTER, PACK], BF16, "codes_last0")
+        interleave(last_q3[:], picked[LAST][:, :, quarter[3]])
+        quantize(mx_tiles("last3", QUARTER), 0, last_q3[:], [(LAST, 3)])
+        scatter(y_sb[1][:], QUARTER, QUARTER)
+        nc.scalar.copy(out=y_sb[2][:, quarter[0]], in_=acc[2][:])
+        products(3, LAST, stop=True)
+        nc.scalar.copy(out=y_sb[2][:, quarter[1]], in_=acc[3][:])
+        scatter(y_sb[2][:], HALF, HALF)
         nc.sync.dma_start(out=out, in_=out_sb[:])

@@ -87,9 +87,9 @@ def tile_list_hboth_none_kernel(
             load_plane(n // PACK, n % PACK)
         nc.sync.dma_start(out=w4_sb[:].bitcast(I32), in_=w4_words.rearrange("a p n -> p a n").bitcast(I32))
         nc.sync.dma_start(out=r8_sb[:].bitcast(I32), in_=r8_words.rearrange("a p n i -> p a (n i)").bitcast(I32))
-        load_scales(nc.sync, r8_scale, r8_scales)
         nc.sync.dma_start(scatter_list[:], offs2)
         nc.sync.dma_start(out=wgo_sb[:], in_=wgo)
+        load_scales(nc.sync, r8_scale, r8_scales)
 
         def list_part(lst, first, count):
             return lst[:, first // LIST_ROWS : (first + count) // LIST_ROWS]

@@ -23,6 +23,8 @@ LAST = PASSES - 1
 HALF = S // 2
 QUARTER = S // 4
 LIST_ROWS = 16
+SHIFT = 32
+ROW = S + 2 * SHIFT
 
 
 def tile_list_hboth_none_kernel(
@@ -34,18 +36,20 @@ def tile_list_hboth_none_kernel(
         psum = ctx.enter_context(tc.psum_pool(name="psum", bufs=1))
 
         def sb(name, shape, dtype, tag=None):
-            return keep.tile(shape, dtype, name=name, tag=tag or name, align_bytes=64)
+            return keep.tile(shape, dtype, name=name, tag=tag or name, align_bytes=256)
 
         gather_list = keep.tile([P, S // LIST_ROWS], U16, name="gather_list")
         scatter_list = keep.tile([P, S // LIST_ROWS], U16, name="scatter_list")
         planes = [[sb(f"plane{a}_{i}", [P, T], F32) for i in range(PACK)] for a in range(PASSES)]
-        picked = [sb(f"picked{a}", [P, PACK * S], F32)[:].rearrange("p (i j) -> p i j", j=S) for a in range(PASSES)]
-        wgt_sb = picked[LAST].rearrange("p i j -> p (i j)")[:, 2 * S + HALF : 3 * S + HALF]
+        picked_tiles = [sb(f"picked{a}", [P, SHIFT + PACK * ROW], F32) for a in range(PASSES)]
+        picked = [t[:, SHIFT:].rearrange("p (i j) -> p i j", j=ROW)[:, :, :S] for t in picked_tiles]
+        wgt_at = 2 * ROW + HALF + 2 * SHIFT
+        wgt_sb = picked_tiles[LAST][:, wgt_at : wgt_at + S]
         wgo_sb = sb("wgo", [P, S], F32)
         w4_sb = sb("w4", [P, PASSES, 2 * M], U8)
         r8_sb = sb("r8", [P, PASSES, PACK * M], U8)
         r8_scale = sb("r8_scale", [P, PASSES, M], U8)
-        tail_a = sb("tail_a", [P, 2, HALF], F32)
+        tail_a = sb("tail_a", [P, SHIFT + S], F32)[:, SHIFT:].rearrange("p (i j) -> p i j", j=HALF)
         early_first = sb("early_first", [P, LAST, QUARTER, PACK], BF16)
         early_rest = sb("early_rest", [P, LAST, S - QUARTER, PACK], BF16)
         last_a = sb("last_a", [P, HALF, PACK], BF16)

@@ -24,7 +24,8 @@ HALF = S // 2
 QUARTER = S // 4
 LIST_ROWS = 16
 SHIFT = 32
-ROW = S + 2 * SHIFT
+ROW = 2 * S
+FIRST = (HALF, HALF + QUARTER, 0, QUARTER)
 
 
 def tile_list_hboth_none_kernel(
@@ -43,16 +44,17 @@ def tile_list_hboth_none_kernel(
         planes = [[sb(f"plane{a}_{i}", [P, T], F32) for i in range(PACK)] for a in range(PASSES)]
         picked_tiles = [sb(f"picked{a}", [P, SHIFT + PACK * ROW], F32) for a in range(PASSES)]
         picked = [t[:, SHIFT:].rearrange("p (i j) -> p i j", j=ROW)[:, :, :S] for t in picked_tiles]
-        wgt_at = 2 * ROW + HALF + 2 * SHIFT
+        wgt_at = 2 * ROW + QUARTER - S
         wgt_sb = picked_tiles[LAST][:, wgt_at : wgt_at + S]
+        tail_at = SHIFT + 3 * ROW + QUARTER
+        tail_a = picked_tiles[LAST][:, tail_at : tail_at + 6 * QUARTER].rearrange("p (i j) -> p i j", i=2)[:, :, :HALF]
         wgo_sb = sb("wgo", [P, S], F32)
         w4_sb = sb("w4", [P, PASSES, 2 * M], U8)
         r8_sb = sb("r8", [P, PASSES, PACK * M], U8)
         r8_scale = sb("r8_scale", [P, PASSES, M], U8)
-        tail_a = sb("tail_a", [P, SHIFT + S], F32)[:, SHIFT:].rearrange("p (i j) -> p i j", j=HALF)
-        early_first = sb("early_first", [P, LAST, QUARTER, PACK], BF16)
-        early_rest = sb("early_rest", [P, LAST, S - QUARTER, PACK], BF16)
-        last_a = sb("last_a", [P, HALF, PACK], BF16)
+        early_first = sb("early_first", [P, S, PACK], BF16)
+        early_rest = sb("early_rest", [P, S, PACK], BF16)
+        last_a = [sb(f"last_q{q}", [P, QUARTER, PACK], BF16) for q in range(2)]
         out_sb = sb("out_sb", [P, T], F32)
         y_sb = [sb("y0", [P, QUARTER], F32), sb("y1", [P, QUARTER], F32), sb("y23", [P, HALF], F32)]
         acc = [psum.tile([P, QUARTER], F32, name=f"acc{q}") for q in range(4)]
@@ -91,9 +93,9 @@ def tile_list_hboth_none_kernel(
             load_plane(n // PACK, n % PACK)
         nc.sync.dma_start(out=w4_sb[:].bitcast(I32), in_=w4_words.rearrange("a p n -> p a n").bitcast(I32))
         nc.sync.dma_start(out=r8_sb[:].bitcast(I32), in_=r8_words.rearrange("a p n i -> p a (n i)").bitcast(I32))
+        load_scales(nc.sync, r8_scale, r8_scales)
         nc.sync.dma_start(scatter_list[:], offs2)
         nc.sync.dma_start(out=wgo_sb[:], in_=wgo)
-        load_scales(nc.sync, r8_scale, r8_scales)
 
         def list_part(lst, first, count):
             return lst[:, first // LIST_ROWS : (first + count) // LIST_ROWS]
@@ -148,54 +150,55 @@ def tile_list_hboth_none_kernel(
                     gather(picked[a][:, i, HALF:], a, i, HALF, HALF)
                 else:
                     gather(picked[a][:, i, :], a, i, 0, S)
-            interleave(early_first[:, a], picked[a][:, :, :QUARTER])
-            interleave(early_rest[:, a], picked[a][:, :, QUARTER:])
+            if a == 0:
+                interleave(early_first[:, : 3 * QUARTER], picked[a][:, :, QUARTER:])
+                interleave(early_rest[:, :QUARTER], picked[a][:, :, :QUARTER])
+            else:
+                interleave(early_first[:, 3 * QUARTER :], picked[a][:, :, quarter[2]])
+                interleave(early_rest[:, QUARTER : 3 * QUARTER], picked[a][:, :, :HALF])
+                interleave(early_rest[:, 3 * QUARTER :], picked[a][:, :, quarter[3]])
         w4_scale = sb("w4_scale", [P, PASSES, M], U8, "plane0_1")
         nc.gpsimd.memset(w4_scale[:].rearrange("p a n -> p (a n)").bitcast(I32), 0)
         load_scales(nc.gpsimd, w4_scale, w4_scales)
 
         gather(picked[LAST][:, 0, :], LAST, 0, 0, S)
-        quantize(
-            mx_tiles("early_first", LAST * QUARTER), 0, early_first[:].rearrange("p a c i -> p (a c) i"), [(0, 0), (1, 0)]
-        )
+        quantize(mx_tiles("early_first", S), 0, early_first[:], [(0, 3), (0, 0), (0, 1), (1, 0)])
         products(0, 0, start=True)
         products(0, 1)
+        products(1, 0, start=True)
+        products(3, 0, start=True)
         gather(picked[LAST][:, 1, :], LAST, 1, 0, S)
-        interleave(last_a[:, :, 0:2], picked[LAST][:, 0:2, :HALF])
-        gather(tail_a[:, 0, :], LAST, 2, 0, HALF)
-        gather(tail_a[:, 1, :], LAST, 3, 0, HALF)
         for q in range(2):
-            interleave(last_a[:, quarter[q], 2:4], tail_a[:, :, quarter[q]])
-        gather(picked[LAST][:, 3, HALF:], LAST, 3, HALF, HALF)
-        gather(picked[LAST][:, 2, HALF:], LAST, 2, HALF, HALF)
-
-        first_tiles = mx_tiles("last0", QUARTER)
-        quantize(first_tiles, 0, last_a[:, quarter[0], :], [(LAST, 0)])
-        quantize(mx_tiles("last1", QUARTER), 0, last_a[:, quarter[1], :], [(LAST, 1)])
+            interleave(last_a[q][:, :, 0:2], picked[LAST][:, 0:2, quarter[2 + q]])
+        gather(tail_a[:, 0, :], LAST, 2, HALF, HALF)
+        gather(tail_a[:, 1, :], LAST, 3, HALF, HALF)
+        for q in range(2):
+            interleave(last_a[q][:, :, 2:4], tail_a[:, :, quarter[q]])
+        gather(picked[LAST][:, 3, quarter[0]], LAST, 3, 0, QUARTER)
+        gather(picked[LAST][:, 2, :HALF], LAST, 2, 0, HALF)
+        last_q2 = sb("last_q2", [P, QUARTER, PACK], BF16)
+        interleave(last_q2[:], picked[LAST][:, :, quarter[0]])
+        quantize(mx_tiles("last0", QUARTER), 0, last_a[0][:], [(LAST, 0)])
+        gather(picked[LAST][:, 3, quarter[1]], LAST, 3, QUARTER, QUARTER)
         products(0, LAST, stop=True)
         nc.scalar.copy(out=y_sb[0][:], in_=acc[0][:])
-        products(1, LAST, start=True)
-        rest_tiles = mx_tiles("early_rest", LAST * (S - QUARTER), "tail_a")
-        for a in range(LAST):
-            quantize(rest_tiles, a * (S - QUARTER), early_rest[:, a], [(a, 1), (a, 2), (a, 3)])
-        products(1, 0)
-        products(1, 1, stop=True)
+        quantize(mx_tiles("early_rest", S, "last_q0"), 0, early_rest[:], [(0, 2), (1, 2), (1, 3), (1, 1)])
+        quantize(mx_tiles("last1", QUARTER), 0, last_a[1][:], [(LAST, 1)])
+        products(1, 1)
+        products(1, LAST, stop=True)
         nc.scalar.copy(out=y_sb[1][:], in_=acc[1][:])
         products(2, 0, start=True)
         products(2, 1)
-        last_q2 = sb("last_q2", [P, QUARTER, PACK], BF16)
-        interleave(last_q2[:], picked[LAST][:, :, quarter[2]])
-        quantize(mx_tiles("last2", QUARTER), 0, last_q2[:], [(LAST, 2)])
-        products(2, LAST, stop=True)
-        products(3, 1, start=True)
-        products(3, 0)
-        scatter(y_sb[0][:], 0, QUARTER)
+        products(3, 1)
+        scatter(y_sb[0][:], FIRST[0], QUARTER)
         last_q3 = sb("last_q3", [P, QUARTER, PACK], BF16, "codes_last0")
-        interleave(last_q3[:], picked[LAST][:, :, quarter[3]])
+        interleave(last_q3[:], picked[LAST][:, :, quarter[1]])
+        quantize(mx_tiles("last2", QUARTER, "picked2"), 0, last_q2[:], [(LAST, 2)])
         quantize(mx_tiles("last3", QUARTER), 0, last_q3[:], [(LAST, 3)])
-        scatter(y_sb[1][:], QUARTER, QUARTER)
+        products(2, LAST, stop=True)
+        scatter(y_sb[1][:], FIRST[1], QUARTER)
         nc.scalar.copy(out=y_sb[2][:, quarter[0]], in_=acc[2][:])
         products(3, LAST, stop=True)
         nc.scalar.copy(out=y_sb[2][:, quarter[1]], in_=acc[3][:])
-        scatter(y_sb[2][:], HALF, HALF)
+        scatter(y_sb[2][:], FIRST[2], HALF)
         nc.sync.dma_start(out=out, in_=out_sb[:])

@@ -52,8 +52,8 @@ def tile_list_hboth_none_kernel(
         w4_sb = sb("w4", [P, PASSES, 2 * M], U8)
         r8_sb = sb("r8", [P, PASSES, PACK * M], U8)
         r8_scale = sb("r8_scale", [P, PASSES, M], U8)
-        early_first = sb("early_first", [P, S, PACK], BF16)
-        early_rest = sb("early_rest", [P, S, PACK], BF16)
+        early_first = sb("early_first", [P, LAST * QUARTER, PACK], BF16)
+        early_rest = sb("early_rest", [P, 3 * LAST * QUARTER, PACK], BF16)
         last_a = [sb(f"last_q{q}", [P, QUARTER, PACK], BF16) for q in range(2)]
         out_sb = sb("out_sb", [P, T], F32)
         y_sb = [sb("y0", [P, QUARTER], F32), sb("y1", [P, QUARTER], F32), sb("y23", [P, HALF], F32)]
@@ -93,9 +93,9 @@ def tile_list_hboth_none_kernel(
             load_plane(n // PACK, n % PACK)
         nc.sync.dma_start(out=w4_sb[:].bitcast(I32), in_=w4_words.rearrange("a p n -> p a n").bitcast(I32))
         nc.sync.dma_start(out=r8_sb[:].bitcast(I32), in_=r8_words.rearrange("a p n i -> p a (n i)").bitcast(I32))
-        load_scales(nc.sync, r8_scale, r8_scales)
         nc.sync.dma_start(scatter_list[:], offs2)
         nc.sync.dma_start(out=wgo_sb[:], in_=wgo)
+        load_scales(nc.sync, r8_scale, r8_scales)
 
         def list_part(lst, first, count):
             return lst[:, first // LIST_ROWS : (first + count) // LIST_ROWS]
@@ -150,23 +150,17 @@ def tile_list_hboth_none_kernel(
                     gather(picked[a][:, i, HALF:], a, i, HALF, HALF)
                 else:
                     gather(picked[a][:, i, :], a, i, 0, S)
-            if a == 0:
-                interleave(early_first[:, : 3 * QUARTER], picked[a][:, :, QUARTER:])
-                interleave(early_rest[:, :QUARTER], picked[a][:, :, :QUARTER])
-            else:
-                interleave(early_first[:, 3 * QUARTER :], picked[a][:, :, quarter[2]])
-                interleave(early_rest[:, QUARTER : 3 * QUARTER], picked[a][:, :, :HALF])
-                interleave(early_rest[:, 3 * QUARTER :], picked[a][:, :, quarter[3]])
+            interleave(early_first[:, quarter[a]], picked[a][:, :, quarter[2]])
+            interleave(early_rest[:, quarter[a]], picked[a][:, :, quarter[3]])
+            interleave(early_rest[:, (a + 1) * HALF : (a + 2) * HALF], picked[a][:, :, :HALF])
         w4_scale = sb("w4_scale", [P, PASSES, M], U8, "plane0_1")
         nc.gpsimd.memset(w4_scale[:].rearrange("p a n -> p (a n)").bitcast(I32), 0)
         load_scales(nc.gpsimd, w4_scale, w4_scales)
 
         gather(picked[LAST][:, 0, :], LAST, 0, 0, S)
-        quantize(mx_tiles("early_first", S), 0, early_first[:], [(0, 3), (0, 0), (0, 1), (1, 0)])
+        quantize(mx_tiles("early_first", LAST * QUARTER), 0, early_first[:], [(0, 0), (1, 0)])
         products(0, 0, start=True)
         products(0, 1)
-        products(1, 0, start=True)
-        products(3, 0, start=True)
         gather(picked[LAST][:, 1, :], LAST, 1, 0, S)
         for q in range(2):
             interleave(last_a[q][:, :, 0:2], picked[LAST][:, 0:2, quarter[2 + q]])
@@ -182,13 +176,17 @@ def tile_list_hboth_none_kernel(
         gather(picked[LAST][:, 3, quarter[1]], LAST, 3, QUARTER, QUARTER)
         products(0, LAST, stop=True)
         nc.scalar.copy(out=y_sb[0][:], in_=acc[0][:])
-        quantize(mx_tiles("early_rest", S, "last_q0"), 0, early_rest[:], [(0, 2), (1, 2), (1, 3), (1, 1)])
+        rest_tiles = mx_tiles("early_rest", 6 * QUARTER, "last_q0")
+        quantize(rest_tiles, 0, early_rest[:, : 3 * QUARTER], [(0, 1), (1, 1), (0, 2)])
         quantize(mx_tiles("last1", QUARTER), 0, last_a[1][:], [(LAST, 1)])
+        quantize(rest_tiles, 3 * QUARTER, early_rest[:, 3 * QUARTER :], [(0, 3), (1, 2), (1, 3)])
+        products(1, 0, start=True)
         products(1, 1)
         products(1, LAST, stop=True)
         nc.scalar.copy(out=y_sb[1][:], in_=acc[1][:])
         products(2, 0, start=True)
         products(2, 1)
+        products(3, 0, start=True)
         products(3, 1)
         scatter(y_sb[0][:], FIRST[0], QUARTER)
         last_q3 = sb("last_q3", [P, QUARTER, PACK], BF16, "codes_last0")

@@ -176,6 +176,17 @@ def tile_list_hboth_none_kernel(
         gather(picked[LAST][:, 3, quarter[1]], LAST, 3, QUARTER, QUARTER)
         products(0, LAST, stop=True)
         nc.scalar.copy(out=y_sb[0][:], in_=acc[0][:])
+        warm = psum.tile([P, HALF], F32, name="warm")
+        for n in range(2):
+            nc.tensor.matmul_mx(
+                out=warm[:, quarter[n]],
+                lhsT=r8_sb[:, LAST, :].bitcast(FP8X4),
+                lhsT_scale=r8_scale[:, LAST, :],
+                rhs=operand[LAST, 0][0].bitcast(FP8X4),
+                rhs_scale=operand[LAST, 0][1],
+                start=True,
+                stop=True,
+            )
         rest_tiles = mx_tiles("early_rest", 6 * QUARTER, "last_q0")
         quantize(rest_tiles, 0, early_rest[:, : 3 * QUARTER], [(0, 1), (1, 1), (0, 2)])
         quantize(mx_tiles("last1", QUARTER), 0, last_a[1][:], [(LAST, 1)])

@@ -1,6 +1,7 @@
 from contextlib import ExitStack
 
 import concourse.mybir as mybir
+from concourse.masks import make_identity
 
 K, M, T, S = 1536, 128, 1024, 512
 FLOPS = 2 * 2 * K * M * S
@@ -14,6 +15,7 @@ U8 = mybir.dt.uint8
 FP8X4 = mybir.dt.float8_e4m3fn_x4
 FP4X4 = mybir.dt.float4_e2m1fn_x4
 MULT = mybir.AluOpType.mult
+COPY = mybir.ActivationFunctionType.Copy
 
 P = 128
 PACK = 4
@@ -23,6 +25,8 @@ LAST = PASSES - 1
 HALF = S // 2
 QUARTER = S // 4
 LIST_ROWS = 16
+GROUPS = P // LIST_ROWS
+CHUNKS = S // P
 SHIFT = 32
 ROW = 2 * S
 FIRST = (HALF, HALF + QUARTER, 0, QUARTER)
@@ -57,10 +61,19 @@ def tile_list_hboth_none_kernel(
         last_a = [sb(f"last_q{q}", [P, QUARTER, PACK], BF16) for q in range(2)]
         out_sb = sb("out_sb", [P, T], F32)
         y_sb = [sb("y0", [P, QUARTER], F32), sb("y1", [P, QUARTER], F32), sb("y23", [P, HALF], F32)]
-        acc = [psum.tile([P, QUARTER], F32, name=f"acc{q}") for q in range(4)]
+        spread = [psum.tile([P, P], F32, name=f"spread{c}", tag=f"acc{c}") for c in range(CHUNKS)]
         wgt_rows = sb("wgt_rows", [P, 32], F32)
         wgt_turned = sb("wgt_turned", [P, 32], F32)
-        wgt_wide = sb("wgt_wide", [P, HALF], F32)
+        wgt_wide = sb("wgt_wide", [P, S], F32)
+        identity = sb("identity", [P, P], F32)
+        raw = sb("raw", [P, S], F32)
+        wgt_columns = sb("wgt_columns", [P, CHUNKS, GROUPS], F32)
+        weighted = sb("weighted", [P, CHUNKS, P], F32)
+        wgt_bank = psum.tile([P, CHUNKS, P], F32, name="wgt_bank", tag="warm")
+        raw_bank = psum.tile([P, CHUNKS, P], F32, name="raw_bank")
+        back_bank = psum.tile([P, CHUNKS, P], F32, name="back_bank")
+
+        make_identity(nc, identity[:])
 
         nc.vector.memset(r8_scale[:].rearrange("p a n -> p (a n)").bitcast(I32), 0)
         nc.vector.memset(out_sb[:], 0.0)
@@ -76,19 +89,18 @@ def tile_list_hboth_none_kernel(
                     in_=scales[:, 4 * quad : 4 * quad + 4, :].rearrange("a r n -> r a n").bitcast(I32),
                 )
 
-        nc.sync.dma_start(out=wgt_rows[:], in_=wgt[0:P:8, :HALF].rearrange("e (b s) -> e b s", s=32))
+        nc.sync.dma_start(out=wgt_rows[:], in_=wgt[0:P:LIST_ROWS, :].rearrange("g (b s) -> b g s", s=32))
         load_plane(0, 0)
         nc.sync.dma_start(gather_list[:], offs)
-        nc.sync.dma_start(out=wgt_sb[:, HALF:], in_=wgt[:, HALF:])
         nc.vector.transpose(wgt_turned[:], wgt_rows[:])
-        wide = wgt_wide[:].rearrange("p (b e r) -> p b e r", e=4, r=8)
-        turned = wgt_turned[:].rearrange("p (e b) -> p b e", e=4)
-        for q in range(2):
-            nc.vector.tensor_copy(
-                out=wide[:, 4 * q : 4 * q + 4], in_=turned[:, 4 * q : 4 * q + 4].unsqueeze(3).to_broadcast([P, 4, 4, 8])
-            )
-        for q in range(2):
-            nc.vector.transpose(wgt_sb[:, q * QUARTER : (q + 1) * QUARTER], wgt_wide[:, q * QUARTER : (q + 1) * QUARTER])
+        wide = wgt_wide[:].rearrange("p (x r) -> p x r", r=LIST_ROWS)
+        for h in range(2):
+            part = slice(16 * h, 16 * h + 16)
+            nc.vector.tensor_copy(out=wide[:, part], in_=wgt_turned[:, part].unsqueeze(2).to_broadcast([P, 16, LIST_ROWS]))
+        wgt_blocks = wgt_sb.rearrange("p (q c s) -> p c q s", c=CHUNKS, s=32)
+        for c in range(CHUNKS):
+            nc.tensor.transpose(spread[c][:], wgt_wide[:, c * P : (c + 1) * P], identity[:])
+            nc.scalar.copy(out=wgt_blocks[:, c], in_=spread[c][:].rearrange("p (q s) -> p q s", s=32))
         for n in range(1, PASSES * PACK):
             load_plane(n // PACK, n % PACK)
         nc.sync.dma_start(out=w4_sb[:].bitcast(I32), in_=w4_words.rearrange("a p n -> p a n").bitcast(I32))
@@ -104,6 +116,22 @@ def tile_list_hboth_none_kernel(
             nc.vector.tensor_tensor(
                 dst, planes[a][i][:].indirect(list_part(gather_list, first, count)), wgt_sb[:, first : first + count], MULT
             )
+
+        def weigh_first_plane():
+            nc.vector.tensor_copy(raw[:], planes[0][0][:].indirect(gather_list[:]))
+            for c in range(CHUNKS):
+                nc.tensor.transpose(wgt_bank[:, c, :], wgt_sb[:, c * P : (c + 1) * P], identity[:])
+            nc.scalar.copy(out=wgt_columns[:], in_=wgt_bank[:, :, 0:P:LIST_ROWS])
+            for c in range(CHUNKS):
+                nc.tensor.transpose(raw_bank[:, c, :], raw[:, c * P : (c + 1) * P], identity[:])
+            for c in range(CHUNKS):
+                for g in range(GROUPS):
+                    rows = slice(g * LIST_ROWS, (g + 1) * LIST_ROWS)
+                    nc.scalar.activation(
+                        out=weighted[:, c, rows], in_=raw_bank[:, c, rows], func=COPY, scale=wgt_columns[:, c, g : g + 1]
+                    )
+                nc.tensor.transpose(back_bank[:, c, :], weighted[:, c, :], identity[:])
+            nc.scalar.copy(out=picked[0][:, 0, :], in_=back_bank[:].rearrange("p c j -> p (c j)"))
 
         def interleave(dst, src):
             nc.scalar.copy(out=dst.rearrange("p (c j) i -> p c i j", j=4), in_=src.rearrange("p i (c j) -> p c i j", j=4))
@@ -146,8 +174,7 @@ def tile_list_hboth_none_kernel(
         for a in range(LAST):
             for i in range(PACK):
                 if (a, i) == (0, 0):
-                    gather(picked[a][:, i, :HALF], a, i, 0, HALF)
-                    gather(picked[a][:, i, HALF:], a, i, HALF, HALF)
+                    weigh_first_plane()
                 else:
                     gather(picked[a][:, i, :], a, i, 0, S)
             interleave(early_first[:, quarter[a]], picked[a][:, :, quarter[2]])
@@ -157,6 +184,7 @@ def tile_list_hboth_none_kernel(
         nc.gpsimd.memset(w4_scale[:].rearrange("p a n -> p (a n)").bitcast(I32), 0)
         load_scales(nc.gpsimd, w4_scale, w4_scales)
 
+        acc = [psum.tile([P, QUARTER], F32, name=f"acc{q}") for q in range(4)]
         gather(picked[LAST][:, 0, :], LAST, 0, 0, S)
         quantize(mx_tiles("early_first", LAST * QUARTER), 0, early_first[:], [(0, 0), (1, 0)])
         products(0, 0, start=True)

@@ -61,20 +61,20 @@ def tile_list_hboth_none_kernel(
         last_a = [sb(f"last_q{q}", [P, QUARTER, PACK], BF16) for q in range(2)]
         out_sb = sb("out_sb", [P, T], F32)
         y_sb = [sb("y0", [P, QUARTER], F32), sb("y1", [P, QUARTER], F32), sb("y23", [P, HALF], F32)]
-        spread = [psum.tile([P, P], F32, name=f"spread{c}", tag=f"acc{c}") for c in range(CHUNKS)]
-        wgt_rows = sb("wgt_rows", [P, 32], F32)
-        wgt_turned = sb("wgt_turned", [P, 32], F32)
+        spread = [psum.tile([P, HALF], F32, name=f"spread{h}", tag=f"acc{h}") for h in range(2)]
+        wgt_rows = sb("wgt_rows", [P, P], F32)
         wgt_wide = sb("wgt_wide", [P, S], F32)
         identity = sb("identity", [P, P], F32)
         raw = sb("raw", [P, S], F32)
-        wgt_columns = sb("wgt_columns", [P, CHUNKS, GROUPS], F32)
+        wgt_columns = sb("wgt_columns", [P, GROUPS, CHUNKS], F32)
         weighted = sb("weighted", [P, CHUNKS, P], F32)
-        wgt_bank = psum.tile([P, CHUNKS, P], F32, name="wgt_bank", tag="warm")
-        raw_bank = psum.tile([P, CHUNKS, P], F32, name="raw_bank")
+        wgt_bank = psum.tile([P, P], F32, name="wgt_bank", tag="warm")
         back_bank = psum.tile([P, CHUNKS, P], F32, name="back_bank")
 
         make_identity(nc, identity[:])
 
+        nc.vector.memset(wgt_rows[32:64], 0.0)
+        nc.vector.memset(wgt_rows[64:], 0.0)
         nc.vector.memset(r8_scale[:].rearrange("p a n -> p (a n)").bitcast(I32), 0)
         nc.vector.memset(out_sb[:], 0.0)
 
@@ -89,18 +89,20 @@ def tile_list_hboth_none_kernel(
                     in_=scales[:, 4 * quad : 4 * quad + 4, :].rearrange("a r n -> r a n").bitcast(I32),
                 )
 
-        nc.sync.dma_start(out=wgt_rows[:], in_=wgt[0:P:LIST_ROWS, :].rearrange("g (b s) -> b g s", s=32))
+        nc.sync.dma_start(out=wgt_rows[:32], in_=wgt[0:P:LIST_ROWS, :].rearrange("g (c j) -> g c j", j=P))
         load_plane(0, 0)
         nc.sync.dma_start(gather_list[:], offs)
-        nc.vector.transpose(wgt_turned[:], wgt_rows[:])
-        wide = wgt_wide[:].rearrange("p (x r) -> p x r", r=LIST_ROWS)
-        for h in range(2):
-            part = slice(16 * h, 16 * h + 16)
-            nc.vector.tensor_copy(out=wide[:, part], in_=wgt_turned[:, part].unsqueeze(2).to_broadcast([P, 16, LIST_ROWS]))
-        wgt_blocks = wgt_sb.rearrange("p (q c s) -> p c q s", c=CHUNKS, s=32)
-        for c in range(CHUNKS):
-            nc.tensor.transpose(spread[c][:], wgt_wide[:, c * P : (c + 1) * P], identity[:])
-            nc.scalar.copy(out=wgt_blocks[:, c], in_=spread[c][:].rearrange("p (q s) -> p q s", s=32))
+        nc.tensor.transpose(wgt_bank[:], wgt_rows[:], identity[:])
+        turned = wgt_bank[:, :32].rearrange("p (g c) -> p c g", c=CHUNKS)
+        wide = wgt_wide[:].rearrange("p (c g r) -> p c g r", c=CHUNKS, r=LIST_ROWS)
+        for h in (1, 0):
+            part = slice(2 * h, 2 * h + 2)
+            nc.scalar.copy(out=wide[:, part], in_=turned[:, part].unsqueeze(3).to_broadcast([P, 2, GROUPS, LIST_ROWS]))
+        for h in (1, 0):
+            for c in range(2):
+                nc.tensor.transpose(spread[h][:, c * P : (c + 1) * P], wgt_wide[:, (2 * h + c) * P : (2 * h + c + 1) * P], identity[:])
+            nc.scalar.copy(out=wgt_sb[:, h * HALF : (h + 1) * HALF], in_=spread[h][:])
+        nc.scalar.copy(out=wgt_columns[:].rearrange("p g c -> p (g c)"), in_=wgt_bank[:, :32])
         for n in range(1, PASSES * PACK):
             load_plane(n // PACK, n % PACK)
         nc.sync.dma_start(out=w4_sb[:].bitcast(I32), in_=w4_words.rearrange("a p n -> p a n").bitcast(I32))
@@ -119,16 +121,14 @@ def tile_list_hboth_none_kernel(
 
         def weigh_first_plane():
             nc.vector.tensor_copy(raw[:], planes[0][0][:].indirect(gather_list[:]))
-            for c in range(CHUNKS):
-                nc.tensor.transpose(wgt_bank[:, c, :], wgt_sb[:, c * P : (c + 1) * P], identity[:])
-            nc.scalar.copy(out=wgt_columns[:], in_=wgt_bank[:, :, 0:P:LIST_ROWS])
+            raw_bank = psum.tile([P, CHUNKS, P], F32, name="raw_bank", tag="acc0")
             for c in range(CHUNKS):
                 nc.tensor.transpose(raw_bank[:, c, :], raw[:, c * P : (c + 1) * P], identity[:])
             for c in range(CHUNKS):
                 for g in range(GROUPS):
                     rows = slice(g * LIST_ROWS, (g + 1) * LIST_ROWS)
                     nc.scalar.activation(
-                        out=weighted[:, c, rows], in_=raw_bank[:, c, rows], func=COPY, scale=wgt_columns[:, c, g : g + 1]
+                        out=weighted[:, c, rows], in_=raw_bank[:, c, rows], func=COPY, scale=wgt_columns[:, g, c : c + 1]
                     )
                 nc.tensor.transpose(back_bank[:, c, :], weighted[:, c, :], identity[:])
             nc.scalar.copy(out=picked[0][:, 0, :], in_=back_bank[:].rearrange("p c j -> p (c j)"))
@@ -175,6 +175,9 @@ def tile_list_hboth_none_kernel(
             for i in range(PACK):
                 if (a, i) == (0, 0):
                     weigh_first_plane()
+                elif (a, i) == (0, 1):
+                    gather(picked[a][:, i, HALF:], a, i, HALF, HALF)
+                    gather(picked[a][:, i, :HALF], a, i, 0, HALF)
                 else:
                     gather(picked[a][:, i, :], a, i, 0, S)
             interleave(early_first[:, quarter[a]], picked[a][:, :, quarter[2]])

@@ -1,7 +1,6 @@
 from contextlib import ExitStack
 
 import concourse.mybir as mybir
-from concourse.masks import make_identity
 
 K, M, T, S = 1536, 128, 1024, 512
 FLOPS = 2 * 2 * K * M * S
@@ -15,6 +14,8 @@ U8 = mybir.dt.uint8
 FP8X4 = mybir.dt.float8_e4m3fn_x4
 FP4X4 = mybir.dt.float4_e2m1fn_x4
 MULT = mybir.AluOpType.mult
+ADD = mybir.AluOpType.add
+EQUAL = mybir.AluOpType.is_equal
 COPY = mybir.ActivationFunctionType.Copy
 
 P = 128
@@ -59,23 +60,31 @@ def tile_list_hboth_none_kernel(
         early_first = sb("early_first", [P, LAST * QUARTER, PACK], BF16)
         early_rest = sb("early_rest", [P, 3 * LAST * QUARTER, PACK], BF16)
         last_a = [sb(f"last_q{q}", [P, QUARTER, PACK], BF16) for q in range(2)]
-        out_sb = sb("out_sb", [P, T], F32)
         y_sb = [sb("y0", [P, QUARTER], F32), sb("y1", [P, QUARTER], F32), sb("y23", [P, HALF], F32)]
         spread = [psum.tile([P, HALF], F32, name=f"spread{h}", tag=f"acc{h}") for h in range(2)]
         wgt_rows = sb("wgt_rows", [P, P], F32)
         wgt_wide = sb("wgt_wide", [P, S], F32)
         identity = sb("identity", [P, P], F32)
-        raw = sb("raw", [P, S], F32)
+        raw = sb("raw", [P, 2, S], F32)
         wgt_columns = sb("wgt_columns", [P, GROUPS, CHUNKS], F32)
-        weighted = sb("weighted", [P, CHUNKS, P], F32)
+        weighted = sb("weighted", [P, CHUNKS, 2, P], F32)
         wgt_bank = psum.tile([P, P], F32, name="wgt_bank", tag="warm")
-        back_bank = psum.tile([P, CHUNKS, P], F32, name="back_bank")
 
-        make_identity(nc, identity[:])
-
+        ones = sb("ones", [P, 32], F32)
+        ramp = sb("ramp", [P, 32], F32)
+        ramp_turned = sb("ramp_turned", [P, 32], F32)
+        nc.vector.memset(ones[:], 1.0)
+        nc.vector.memset(identity[:], 0.0)
+        nc.vector.tensor_tensor_scan(ramp[:], ones[:], ones[:], 0.0, MULT, ADD)
         nc.vector.memset(wgt_rows[32:64], 0.0)
+        nc.vector.transpose(ramp_turned[:], ramp[:])
         nc.vector.memset(wgt_rows[64:], 0.0)
+        for quad in range(4):
+            block = slice(32 * quad, 32 * quad + 32)
+            nc.vector.tensor_tensor(identity[block, block], ramp[block], ramp_turned[block], EQUAL)
+
         nc.vector.memset(r8_scale[:].rearrange("p a n -> p (a n)").bitcast(I32), 0)
+        out_sb = sb("out_sb", [P, T], F32, "ramp_turned")
         nc.vector.memset(out_sb[:], 0.0)
 
         def load_plane(a, i):
@@ -119,19 +128,24 @@ def tile_list_hboth_none_kernel(
                 dst, planes[a][i][:].indirect(list_part(gather_list, first, count)), wgt_sb[:, first : first + count], MULT
             )
 
-        def weigh_first_plane():
-            nc.vector.tensor_copy(raw[:], planes[0][0][:].indirect(gather_list[:]))
-            raw_bank = psum.tile([P, CHUNKS, P], F32, name="raw_bank", tag="acc0")
-            for c in range(CHUNKS):
-                nc.tensor.transpose(raw_bank[:, c, :], raw[:, c * P : (c + 1) * P], identity[:])
-            for c in range(CHUNKS):
+        def weigh(h, count, tag):
+            raw_bank = psum.tile([P, 2, count, P], F32, name=f"raw_bank{h}", tag=tag)
+            back_bank = psum.tile([P, count, HALF], F32, name=f"back_bank{h}")
+            for i in reversed(range(count)):
+                for c in range(2):
+                    nc.tensor.transpose(raw_bank[:, c, i, :], raw[:, i, quarter[2 * h + c]], identity[:])
+            for c in range(2):
                 for g in range(GROUPS):
                     rows = slice(g * LIST_ROWS, (g + 1) * LIST_ROWS)
                     nc.scalar.activation(
-                        out=weighted[:, c, rows], in_=raw_bank[:, c, rows], func=COPY, scale=wgt_columns[:, g, c : c + 1]
+                        out=weighted[:, 2 * h + c, :count, rows],
+                        in_=raw_bank[:, c, :, rows],
+                        func=COPY,
+                        scale=wgt_columns[:, g, 2 * h + c : 2 * h + c + 1],
                     )
-                nc.tensor.transpose(back_bank[:, c, :], weighted[:, c, :], identity[:])
-            nc.scalar.copy(out=picked[0][:, 0, :], in_=back_bank[:].rearrange("p c j -> p (c j)"))
+                for i in range(count):
+                    nc.tensor.transpose(back_bank[:, i, quarter[c]], weighted[:, 2 * h + c, i, :], identity[:])
+            nc.scalar.copy(out=picked[0][:, :count, h * HALF : (h + 1) * HALF], in_=back_bank[:])
 
         def interleave(dst, src):
             nc.scalar.copy(out=dst.rearrange("p (c j) i -> p c i j", j=4), in_=src.rearrange("p i (c j) -> p c i j", j=4))
@@ -174,10 +188,12 @@ def tile_list_hboth_none_kernel(
         for a in range(LAST):
             for i in range(PACK):
                 if (a, i) == (0, 0):
-                    weigh_first_plane()
+                    nc.vector.tensor_copy(raw[:, 0, :], planes[0][0][:].indirect(gather_list[:]))
+                    weigh(1, 1, "acc0")
                 elif (a, i) == (0, 1):
+                    nc.vector.tensor_copy(raw[:, 1, :HALF], planes[0][1][:].indirect(list_part(gather_list, 0, HALF)))
                     gather(picked[a][:, i, HALF:], a, i, HALF, HALF)
-                    gather(picked[a][:, i, :HALF], a, i, 0, HALF)
+                    weigh(0, 2, "acc1")
                 else:
                     gather(picked[a][:, i, :], a, i, 0, S)
             interleave(early_first[:, quarter[a]], picked[a][:, :, quarter[2]])

@@ -1,6 +1,7 @@
 from contextlib import ExitStack
 
 import concourse.mybir as mybir
+from concourse.masks import make_identity
 
 K, M, T, S = 1536, 128, 1024, 512
 FLOPS = 2 * 2 * K * M * S
@@ -14,8 +15,6 @@ U8 = mybir.dt.uint8
 FP8X4 = mybir.dt.float8_e4m3fn_x4
 FP4X4 = mybir.dt.float4_e2m1fn_x4
 MULT = mybir.AluOpType.mult
-ADD = mybir.AluOpType.add
-EQUAL = mybir.AluOpType.is_equal
 COPY = mybir.ActivationFunctionType.Copy
 
 P = 128
@@ -70,21 +69,13 @@ def tile_list_hboth_none_kernel(
         weighted = sb("weighted", [P, CHUNKS, 2, P], F32)
         wgt_bank = psum.tile([P, P], F32, name="wgt_bank", tag="warm")
 
-        ones = sb("ones", [P, 32], F32)
-        ramp = sb("ramp", [P, 32], F32)
-        ramp_turned = sb("ramp_turned", [P, 32], F32)
-        nc.vector.memset(ones[:], 1.0)
-        nc.vector.memset(identity[:], 0.0)
-        nc.vector.tensor_tensor_scan(ramp[:], ones[:], ones[:], 0.0, MULT, ADD)
-        nc.vector.memset(wgt_rows[32:64], 0.0)
-        nc.vector.transpose(ramp_turned[:], ramp[:])
-        nc.vector.memset(wgt_rows[64:], 0.0)
-        for quad in range(4):
-            block = slice(32 * quad, 32 * quad + 32)
-            nc.vector.tensor_tensor(identity[block, block], ramp[block], ramp_turned[block], EQUAL)
+        out_sb = sb("out_sb", [P, T], F32)
 
+        make_identity(nc, identity[:])
+
+        nc.vector.memset(wgt_rows[32:64], 0.0)
+        nc.vector.memset(wgt_rows[64:], 0.0)
         nc.vector.memset(r8_scale[:].rearrange("p a n -> p (a n)").bitcast(I32), 0)
-        out_sb = sb("out_sb", [P, T], F32, "ramp_turned")
         nc.vector.memset(out_sb[:], 0.0)
 
         def load_plane(a, i):
@@ -99,8 +90,8 @@ def tile_list_hboth_none_kernel(
                 )
 
         nc.sync.dma_start(out=wgt_rows[:32], in_=wgt[0:P:LIST_ROWS, :].rearrange("g (c j) -> g c j", j=P))
-        load_plane(0, 0)
         nc.sync.dma_start(gather_list[:], offs)
+        load_plane(0, 0)
         nc.tensor.transpose(wgt_bank[:], wgt_rows[:], identity[:])
         turned = wgt_bank[:, :32].rearrange("p (g c) -> p c g", c=CHUNKS)
         wide = wgt_wide[:].rearrange("p (c g r) -> p c g r", c=CHUNKS, r=LIST_ROWS)
@@ -117,8 +108,9 @@ def tile_list_hboth_none_kernel(
         nc.sync.dma_start(out=w4_sb[:].bitcast(I32), in_=w4_words.rearrange("a p n -> p a n").bitcast(I32))
         nc.sync.dma_start(out=r8_sb[:].bitcast(I32), in_=r8_words.rearrange("a p n i -> p a (n i)").bitcast(I32))
         nc.sync.dma_start(scatter_list[:], offs2)
-        nc.sync.dma_start(out=wgo_sb[:], in_=wgo)
+        nc.sync.dma_start(out=wgo_sb[:, HALF:], in_=wgo[:, HALF:])
         load_scales(nc.sync, r8_scale, r8_scales)
+        nc.sync.dma_start(out=wgo_sb[:, :HALF], in_=wgo[:, :HALF])
 
         def list_part(lst, first, count):
             return lst[:, first // LIST_ROWS : (first + count) // LIST_ROWS]

@@ -27,6 +27,7 @@ QUARTER = S // 4
 LIST_ROWS = 16
 GROUPS = P // LIST_ROWS
 CHUNKS = S // P
+CHUNK_ORDER = (2, 3, 0, 1)
 SHIFT = 32
 ROW = 2 * S
 FIRST = (HALF, HALF + QUARTER, 0, QUARTER)
@@ -60,13 +61,14 @@ def tile_list_hboth_none_kernel(
         early_rest = sb("early_rest", [P, 3 * LAST * QUARTER, PACK], BF16)
         last_a = [sb(f"last_q{q}", [P, QUARTER, PACK], BF16) for q in range(2)]
         y_sb = [sb("y0", [P, QUARTER], F32), sb("y1", [P, QUARTER], F32), sb("y23", [P, HALF], F32)]
-        spread = [psum.tile([P, HALF], F32, name=f"spread{h}", tag=f"acc{h}") for h in range(2)]
+        spread = [psum.tile([P, P], F32, name=f"spread{c}", tag=f"acc{c}") for c in range(CHUNKS)]
         wgt_rows = sb("wgt_rows", [P, P], F32)
         wgt_wide = sb("wgt_wide", [P, S], F32)
         identity = sb("identity", [P, P], F32)
         raw = sb("raw", [P, 2, S], F32)
         wgt_columns = sb("wgt_columns", [P, GROUPS, CHUNKS], F32)
-        weighted = sb("weighted", [P, CHUNKS, 2, P], F32)
+        weighted = sb("weighted", [P, CHUNKS, P, 2], BF16)
+        pairs = sb("pairs", [P, 2, S], F32)
         wgt_bank = psum.tile([P, P], F32, name="wgt_bank", tag="warm")
 
         out_sb = sb("out_sb", [P, T], F32)
@@ -89,19 +91,17 @@ def tile_list_hboth_none_kernel(
                     in_=scales[:, 4 * quad : 4 * quad + 4, :].rearrange("a r n -> r a n").bitcast(I32),
                 )
 
-        nc.sync.dma_start(out=wgt_rows[:32], in_=wgt[0:P:LIST_ROWS, :].rearrange("g (c j) -> g c j", j=P))
-        nc.sync.dma_start(gather_list[:], offs)
         load_plane(0, 0)
+        nc.sync.dma_start(gather_list[:], offs)
+        nc.sync.dma_start(out=wgt_rows[:32], in_=wgt[0:P:LIST_ROWS, :].rearrange("g (c j) -> g c j", j=P))
         nc.tensor.transpose(wgt_bank[:], wgt_rows[:], identity[:])
         turned = wgt_bank[:, :32].rearrange("p (g c) -> p c g", c=CHUNKS)
         wide = wgt_wide[:].rearrange("p (c g r) -> p c g r", c=CHUNKS, r=LIST_ROWS)
-        for h in (1, 0):
-            part = slice(2 * h, 2 * h + 2)
-            nc.scalar.copy(out=wide[:, part], in_=turned[:, part].unsqueeze(3).to_broadcast([P, 2, GROUPS, LIST_ROWS]))
-        for h in (1, 0):
-            for c in range(2):
-                nc.tensor.transpose(spread[h][:, c * P : (c + 1) * P], wgt_wide[:, (2 * h + c) * P : (2 * h + c + 1) * P], identity[:])
-            nc.scalar.copy(out=wgt_sb[:, h * HALF : (h + 1) * HALF], in_=spread[h][:])
+        for c in CHUNK_ORDER:
+            nc.scalar.copy(out=wide[:, c], in_=turned[:, c].unsqueeze(2).to_broadcast([P, GROUPS, LIST_ROWS]))
+        for c in CHUNK_ORDER:
+            nc.tensor.transpose(spread[c][:], wgt_wide[:, c * P : (c + 1) * P], identity[:])
+            nc.scalar.copy(out=wgt_sb[:, c * P : (c + 1) * P], in_=spread[c][:])
         nc.scalar.copy(out=wgt_columns[:].rearrange("p g c -> p (g c)"), in_=wgt_bank[:, :32])
         for n in range(1, PASSES * PACK):
             load_plane(n // PACK, n % PACK)
@@ -120,24 +120,28 @@ def tile_list_hboth_none_kernel(
                 dst, planes[a][i][:].indirect(list_part(gather_list, first, count)), wgt_sb[:, first : first + count], MULT
             )
 
-        def weigh(h, count, tag):
-            raw_bank = psum.tile([P, 2, count, P], F32, name=f"raw_bank{h}", tag=tag)
-            back_bank = psum.tile([P, count, HALF], F32, name=f"back_bank{h}")
-            for i in reversed(range(count)):
+        def weigh(h, tag):
+            raw_bank = psum.tile([P, 2, 2, P], F32, name=f"raw_bank{h}", tag=tag)
+            back_bank = psum.tile([P, HALF], F32, name=f"back_bank{h}")
+            for i in (1, 0):
                 for c in range(2):
                     nc.tensor.transpose(raw_bank[:, c, i, :], raw[:, i, quarter[2 * h + c]], identity[:])
             for c in range(2):
                 for g in range(GROUPS):
                     rows = slice(g * LIST_ROWS, (g + 1) * LIST_ROWS)
                     nc.scalar.activation(
-                        out=weighted[:, 2 * h + c, :count, rows],
-                        in_=raw_bank[:, c, :, rows],
+                        out=weighted[:, 2 * h + c, rows, :],
+                        in_=raw_bank[:, c, :, rows].rearrange("p i r -> p r i"),
                         func=COPY,
                         scale=wgt_columns[:, g, 2 * h + c : 2 * h + c + 1],
                     )
-                for i in range(count):
-                    nc.tensor.transpose(back_bank[:, i, quarter[c]], weighted[:, 2 * h + c, i, :], identity[:])
-            nc.scalar.copy(out=picked[0][:, :count, h * HALF : (h + 1) * HALF], in_=back_bank[:])
+                words = weighted[:, 2 * h + c].rearrange("p r i -> p (r i)").bitcast(F32)
+                nc.tensor.transpose(back_bank[:, quarter[c]], words, identity[:])
+            nc.scalar.copy(out=pairs[:, 0, h * HALF : (h + 1) * HALF], in_=back_bank[:])
+
+        def join(dst, places):
+            words = dst.rearrange("p n i -> p (n i)").bitcast(U32).rearrange("p (c j u) -> p c u j", j=4, u=2)
+            nc.scalar.copy(out=words, in_=pairs[:, :, places].bitcast(U32).rearrange("p u (c j) -> p c u j", j=4))
 
         def interleave(dst, src):
             nc.scalar.copy(out=dst.rearrange("p (c j) i -> p c i j", j=4), in_=src.rearrange("p i (c j) -> p c i j", j=4))
@@ -179,15 +183,21 @@ def tile_list_hboth_none_kernel(
         quarter = [slice(q * QUARTER, (q + 1) * QUARTER) for q in range(4)]
         for a in range(LAST):
             for i in range(PACK):
-                if (a, i) == (0, 0):
-                    nc.vector.tensor_copy(raw[:, 0, :], planes[0][0][:].indirect(gather_list[:]))
-                    weigh(1, 1, "acc0")
-                elif (a, i) == (0, 1):
-                    nc.vector.tensor_copy(raw[:, 1, :HALF], planes[0][1][:].indirect(list_part(gather_list, 0, HALF)))
+                if a == 0 and i < 2:
+                    nc.vector.tensor_copy(raw[:, i, :], planes[0][i][:].indirect(gather_list[:]))
+                elif (a, i) == (0, 2):
+                    weigh(1, "acc2")
+                    weigh(0, "acc3")
                     gather(picked[a][:, i, HALF:], a, i, HALF, HALF)
-                    weigh(0, 2, "acc1")
+                    gather(picked[a][:, i, :HALF], a, i, 0, HALF)
                 else:
                     gather(picked[a][:, i, :], a, i, 0, S)
+            if a == 0:
+                interleave(pairs[:, 1, :].bitcast(BF16).rearrange("p (n i) -> p n i", i=2), picked[a][:, 2:4, :])
+                join(early_first[:, quarter[a]], quarter[2])
+                join(early_rest[:, quarter[a]], quarter[3])
+                join(early_rest[:, (a + 1) * HALF : (a + 2) * HALF], slice(0, HALF))
+                continue
             interleave(early_first[:, quarter[a]], picked[a][:, :, quarter[2]])
             interleave(early_rest[:, quarter[a]], picked[a][:, :, quarter[3]])
             interleave(early_rest[:, (a + 1) * HALF : (a + 2) * HALF], picked[a][:, :, :HALF])

@@ -15,6 +15,7 @@ U8 = mybir.dt.uint8
 FP8X4 = mybir.dt.float8_e4m3fn_x4
 FP4X4 = mybir.dt.float4_e2m1fn_x4
 MULT = mybir.AluOpType.mult
+ADD = mybir.AluOpType.add
 COPY = mybir.ActivationFunctionType.Copy
 
 P = 128
@@ -75,10 +76,15 @@ def tile_list_hboth_none_kernel(
 
         make_identity(nc, identity[:])
 
-        nc.vector.memset(wgt_rows[32:64], 0.0)
-        nc.vector.memset(wgt_rows[64:], 0.0)
-        nc.vector.memset(r8_scale[:].rearrange("p a n -> p (a n)").bitcast(I32), 0)
-        nc.vector.memset(out_sb[:], 0.0)
+        def clear(words, zero):
+            cut = words.shape[1] // 2 + 1
+            nc.vector.memset(words[:, :cut], zero)
+            nc.vector.memset(words[:, cut:], zero)
+
+        clear(out_sb[:], 0.0)
+        clear(wgt_rows[32:64], 0.0)
+        clear(wgt_rows[64:], 0.0)
+        clear(r8_scale[:].rearrange("p a n -> p (a n)").bitcast(I32), 0)
 
         def load_plane(a, i):
             rows = xT[a * K_PASS : (a + 1) * K_PASS, :].rearrange("(p i) t -> p i t", i=PACK)
@@ -123,7 +129,7 @@ def tile_list_hboth_none_kernel(
         def weigh(h, tag):
             raw_bank = psum.tile([P, 2, 2, P], F32, name=f"raw_bank{h}", tag=tag)
             back_bank = psum.tile([P, HALF], F32, name=f"back_bank{h}")
-            for i in (1, 0):
+            for i in range(2):
                 for c in range(2):
                     nc.tensor.transpose(raw_bank[:, c, i, :], raw[:, i, quarter[2 * h + c]], identity[:])
             for c in range(2):
@@ -184,7 +190,7 @@ def tile_list_hboth_none_kernel(
         for a in range(LAST):
             for i in range(PACK):
                 if a == 0 and i < 2:
-                    nc.vector.tensor_copy(raw[:, i, :], planes[0][i][:].indirect(gather_list[:]))
+                    nc.vector.tensor_tensor(raw[:, i, :], planes[0][i][:].indirect(gather_list[:]), out_sb[:, :S], ADD)
                 elif (a, i) == (0, 2):
                     weigh(1, "acc2")
                     weigh(0, "acc3")

@@ -15,7 +15,6 @@ U8 = mybir.dt.uint8
 FP8X4 = mybir.dt.float8_e4m3fn_x4
 FP4X4 = mybir.dt.float4_e2m1fn_x4
 MULT = mybir.AluOpType.mult
-ADD = mybir.AluOpType.add
 COPY = mybir.ActivationFunctionType.Copy
 
 P = 128
@@ -28,10 +27,7 @@ QUARTER = S // 4
 LIST_ROWS = 16
 GROUPS = P // LIST_ROWS
 CHUNKS = S // P
-CHUNK_ORDER = (2, 3, 0, 1)
-SHIFT = 32
-ROW = 2 * S
-FIRST = (HALF, HALF + QUARTER, 0, QUARTER)
+WHOLE, LATEST, LATE, FINAL = 1, 0, 3, 2
 
 
 def tile_list_hboth_none_kernel(
@@ -45,46 +41,43 @@ def tile_list_hboth_none_kernel(
         def sb(name, shape, dtype, tag=None):
             return keep.tile(shape, dtype, name=name, tag=tag or name, align_bytes=256)
 
+        quarter = [slice(q * QUARTER, (q + 1) * QUARTER) for q in range(4)]
+        half = [slice(h * HALF, (h + 1) * HALF) for h in range(2)]
+
         gather_list = keep.tile([P, S // LIST_ROWS], U16, name="gather_list")
         scatter_list = keep.tile([P, S // LIST_ROWS], U16, name="scatter_list")
         planes = [[sb(f"plane{a}_{i}", [P, T], F32) for i in range(PACK)] for a in range(PASSES)]
-        picked_tiles = [sb(f"picked{a}", [P, SHIFT + PACK * ROW], F32) for a in range(PASSES)]
-        picked = [t[:, SHIFT:].rearrange("p (i j) -> p i j", j=ROW)[:, :, :S] for t in picked_tiles]
-        wgt_at = 2 * ROW + QUARTER - S
-        wgt_sb = picked_tiles[LAST][:, wgt_at : wgt_at + S]
-        tail_at = SHIFT + 3 * ROW + QUARTER
-        tail_a = picked_tiles[LAST][:, tail_at : tail_at + 6 * QUARTER].rearrange("p (i j) -> p i j", i=2)[:, :, :HALF]
+        raw = sb("raw", [P, 2, S], F32)
+        picked0 = sb("picked0", [P, 2, S], F32)
+        picked1 = sb("picked1", [P, PACK, S], F32)
+        picked2 = sb("picked2", [P, 14 * HALF], F32)
+        first_half = picked2[:, : 8 * HALF].rearrange("p (i j) -> p i j", i=PACK)[:, :, :HALF]
+        second_half = picked2[:].rearrange("p (u r j) -> p u r j", u=2, r=7)[:, :, 0:4:3, :]
+        wgt_sb = picked2[:, 10 * HALF : 12 * HALF]
         wgo_sb = sb("wgo", [P, S], F32)
         w4_sb = sb("w4", [P, PASSES, 2 * M], U8)
         r8_sb = sb("r8", [P, PASSES, PACK * M], U8)
         r8_scale = sb("r8_scale", [P, PASSES, M], U8)
-        early_first = sb("early_first", [P, LAST * QUARTER, PACK], BF16)
-        early_rest = sb("early_rest", [P, 3 * LAST * QUARTER, PACK], BF16)
-        last_a = [sb(f"last_q{q}", [P, QUARTER, PACK], BF16) for q in range(2)]
-        y_sb = [sb("y0", [P, QUARTER], F32), sb("y1", [P, QUARTER], F32), sb("y23", [P, HALF], F32)]
+        early = [sb(f"early{n}", [P, S, PACK], BF16) for n in range(2)]
+        last = [sb(f"last{q}", [P, QUARTER, PACK], BF16) for q in range(2)]
+        y_first = sb("y_first", [P, QUARTER], F32)
+        y_second = picked2[:, quarter[0]]
+        y_rest = sb("y_rest", [P, HALF], F32)
         spread = [psum.tile([P, P], F32, name=f"spread{c}", tag=f"acc{c}") for c in range(CHUNKS)]
         wgt_rows = sb("wgt_rows", [P, P], F32)
         wgt_wide = sb("wgt_wide", [P, S], F32)
         identity = sb("identity", [P, P], F32)
-        raw = sb("raw", [P, 2, S], F32)
         wgt_columns = sb("wgt_columns", [P, GROUPS, CHUNKS], F32)
         weighted = sb("weighted", [P, CHUNKS, P, 2], BF16)
         pairs = sb("pairs", [P, 2, S], F32)
-        wgt_bank = psum.tile([P, P], F32, name="wgt_bank", tag="warm")
-
+        wgt_bank = psum.tile([P, P], F32, name="wgt_bank")
         out_sb = sb("out_sb", [P, T], F32)
 
         make_identity(nc, identity[:])
-
-        def clear(words, zero):
-            cut = words.shape[1] // 2 + 1
-            nc.vector.memset(words[:, :cut], zero)
-            nc.vector.memset(words[:, cut:], zero)
-
-        clear(out_sb[:], 0.0)
-        clear(wgt_rows[32:64], 0.0)
-        clear(wgt_rows[64:], 0.0)
-        clear(r8_scale[:].rearrange("p a n -> p (a n)").bitcast(I32), 0)
+        nc.vector.memset(wgt_rows[32:64], 0.0)
+        nc.vector.memset(wgt_rows[64:], 0.0)
+        nc.vector.memset(r8_scale[:].rearrange("p a n -> p (a n)").bitcast(I32), 0)
+        nc.vector.memset(out_sb[:], 0.0)
 
         def load_plane(a, i):
             rows = xT[a * K_PASS : (a + 1) * K_PASS, :].rearrange("(p i) t -> p i t", i=PACK)
@@ -103,31 +96,31 @@ def tile_list_hboth_none_kernel(
         nc.tensor.transpose(wgt_bank[:], wgt_rows[:], identity[:])
         turned = wgt_bank[:, :32].rearrange("p (g c) -> p c g", c=CHUNKS)
         wide = wgt_wide[:].rearrange("p (c g r) -> p c g r", c=CHUNKS, r=LIST_ROWS)
-        for c in CHUNK_ORDER:
+        for c in range(CHUNKS):
             nc.scalar.copy(out=wide[:, c], in_=turned[:, c].unsqueeze(2).to_broadcast([P, GROUPS, LIST_ROWS]))
-        for c in CHUNK_ORDER:
-            nc.tensor.transpose(spread[c][:], wgt_wide[:, c * P : (c + 1) * P], identity[:])
-            nc.scalar.copy(out=wgt_sb[:, c * P : (c + 1) * P], in_=spread[c][:])
+        for c in range(CHUNKS):
+            nc.tensor.transpose(spread[c][:], wgt_wide[:, quarter[c]], identity[:])
+            nc.scalar.copy(out=wgt_sb[:, quarter[c]], in_=spread[c][:])
         nc.scalar.copy(out=wgt_columns[:].rearrange("p g c -> p (g c)"), in_=wgt_bank[:, :32])
-        for n in range(1, PASSES * PACK):
+        for n in range(1, LAST * PACK):
             load_plane(n // PACK, n % PACK)
-        nc.sync.dma_start(out=w4_sb[:].bitcast(I32), in_=w4_words.rearrange("a p n -> p a n").bitcast(I32))
+        for i in (WHOLE, LATEST, LATE, FINAL):
+            load_plane(LAST, i)
         nc.sync.dma_start(out=r8_sb[:].bitcast(I32), in_=r8_words.rearrange("a p n i -> p a (n i)").bitcast(I32))
+        nc.sync.dma_start(out=w4_sb[:].bitcast(I32), in_=w4_words.rearrange("a p n -> p a n").bitcast(I32))
         nc.sync.dma_start(scatter_list[:], offs2)
-        nc.sync.dma_start(out=wgo_sb[:, HALF:], in_=wgo[:, HALF:])
         load_scales(nc.sync, r8_scale, r8_scales)
-        nc.sync.dma_start(out=wgo_sb[:, :HALF], in_=wgo[:, :HALF])
+        for h in range(2):
+            nc.sync.dma_start(out=wgo_sb[:, half[h]], in_=wgo[:, half[h]])
 
-        def list_part(lst, first, count):
-            return lst[:, first // LIST_ROWS : (first + count) // LIST_ROWS]
+        def list_part(lst, places):
+            return lst[:, places.start // LIST_ROWS : places.stop // LIST_ROWS]
 
-        def gather(dst, a, i, first, count):
-            nc.vector.tensor_tensor(
-                dst, planes[a][i][:].indirect(list_part(gather_list, first, count)), wgt_sb[:, first : first + count], MULT
-            )
+        def gather(dst, a, i, places):
+            nc.vector.tensor_tensor(dst, planes[a][i][:].indirect(list_part(gather_list, places)), wgt_sb[:, places], MULT)
 
-        def weigh(h, tag):
-            raw_bank = psum.tile([P, 2, 2, P], F32, name=f"raw_bank{h}", tag=tag)
+        def weigh(h):
+            raw_bank = psum.tile([P, 2, 2, P], F32, name=f"raw_bank{h}", tag=f"acc{h}")
             back_bank = psum.tile([P, HALF], F32, name=f"back_bank{h}")
             for i in range(2):
                 for c in range(2):
@@ -143,7 +136,7 @@ def tile_list_hboth_none_kernel(
                     )
                 words = weighted[:, 2 * h + c].rearrange("p r i -> p (r i)").bitcast(F32)
                 nc.tensor.transpose(back_bank[:, quarter[c]], words, identity[:])
-            nc.scalar.copy(out=pairs[:, 0, h * HALF : (h + 1) * HALF], in_=back_bank[:])
+            nc.scalar.copy(out=pairs[:, 0, half[h]], in_=back_bank[:])
 
         def join(dst, places):
             words = dst.rearrange("p n i -> p (n i)").bitcast(U32).rearrange("p (c j u) -> p c u j", j=4, u=2)
@@ -152,21 +145,23 @@ def tile_list_hboth_none_kernel(
         def interleave(dst, src):
             nc.scalar.copy(out=dst.rearrange("p (c j) i -> p c i j", j=4), in_=src.rearrange("p i (c j) -> p c i j", j=4))
 
+        def interleave_second(q):
+            nc.scalar.copy(
+                out=last_rest[:, quarter[q]].rearrange("p (c j) (u v) -> p c u v j", j=4, u=2),
+                in_=second_half[:, :, :, quarter[q]].rearrange("p u v (c j) -> p c u v j", j=4),
+            )
+
         operand = {}
 
-        def mx_tiles(name, width, tag=None):
-            return sb(f"codes_{name}", [P, width], U32, tag), sb(f"scales_{name}", [P, width], U8)
-
-        def quantize(tiles, first, grouped, keys):
-            cols = slice(first, first + len(keys) * QUARTER)
-            nc.vector.quantize_mx(
-                out=tiles[0][:, cols].bitcast(FP8X4), scales=tiles[1][:, cols], in_=grouped.rearrange("p c i -> p (c i)")
-            )
+        def quantize(name, grouped, keys, tag=None):
+            width = len(keys) * QUARTER
+            codes = sb(f"codes_{name}", [P, width], U32, tag)
+            scales = sb(f"scales_{name}", [P, width], U8)
+            nc.vector.quantize_mx(out=codes[:].bitcast(FP8X4), scales=scales[:], in_=grouped.rearrange("p c i -> p (c i)"))
             for n, key in enumerate(keys):
-                part = slice(first + n * QUARTER, first + (n + 1) * QUARTER)
-                operand[key] = (tiles[0][:, part], tiles[1][:, part])
+                operand[key] = (codes[:, quarter[n]], scales[:, quarter[n]])
 
-        def products(q, a, start=False, stop=False):
+        def products(q, a):
             codes, scales = operand[a, q]
             for n, (lhs, lhs_scale) in enumerate(
                 ((r8_sb[:, a, :].bitcast(FP8X4), r8_scale), (w4_sb[:, a, :].bitcast(FP4X4), w4_scale))
@@ -177,92 +172,68 @@ def tile_list_hboth_none_kernel(
                     lhsT_scale=lhs_scale[:, a, :],
                     rhs=codes.bitcast(FP8X4),
                     rhs_scale=scales,
-                    start=start and n == 0,
-                    stop=stop and n == 1,
+                    start=(a, n) == (0, 0),
+                    stop=(a, n) == (LAST, 1),
                 )
 
-        def scatter(values, first, count):
-            nc.vector.tensor_tensor(
-                out_sb[:].indirect(list_part(scatter_list, first, count)), values, wgo_sb[:, first : first + count], MULT
-            )
+        def scatter(values, places):
+            nc.vector.tensor_tensor(out_sb[:].indirect(list_part(scatter_list, places)), values, wgo_sb[:, places], MULT)
 
-        quarter = [slice(q * QUARTER, (q + 1) * QUARTER) for q in range(4)]
-        for a in range(LAST):
-            for i in range(PACK):
-                if a == 0 and i < 2:
-                    nc.vector.tensor_tensor(raw[:, i, :], planes[0][i][:].indirect(gather_list[:]), out_sb[:, :S], ADD)
-                elif (a, i) == (0, 2):
-                    weigh(1, "acc2")
-                    weigh(0, "acc3")
-                    gather(picked[a][:, i, HALF:], a, i, HALF, HALF)
-                    gather(picked[a][:, i, :HALF], a, i, 0, HALF)
-                else:
-                    gather(picked[a][:, i, :], a, i, 0, S)
-            if a == 0:
-                interleave(pairs[:, 1, :].bitcast(BF16).rearrange("p (n i) -> p n i", i=2), picked[a][:, 2:4, :])
-                join(early_first[:, quarter[a]], quarter[2])
-                join(early_rest[:, quarter[a]], quarter[3])
-                join(early_rest[:, (a + 1) * HALF : (a + 2) * HALF], slice(0, HALF))
-                continue
-            interleave(early_first[:, quarter[a]], picked[a][:, :, quarter[2]])
-            interleave(early_rest[:, quarter[a]], picked[a][:, :, quarter[3]])
-            interleave(early_rest[:, (a + 1) * HALF : (a + 2) * HALF], picked[a][:, :, :HALF])
+        whole = slice(0, S)
+        for i in range(2):
+            nc.vector.tensor_copy(raw[:, i, :], planes[0][i][:].indirect(gather_list[:]))
+        weigh(0)
+        weigh(1)
+        for h in range(2):
+            gather(picked0[:, 0, half[h]], 0, 2, half[h])
+        gather(picked0[:, 1, :], 0, 3, whole)
+        interleave(pairs[:, 1, :].bitcast(BF16).rearrange("p (n i) -> p n i", i=2), picked0[:])
+        join(early[0][:, : 3 * QUARTER], slice(0, 3 * QUARTER))
+        join(early[1][:, quarter[3]], quarter[3])
+        for i in range(PACK):
+            gather(picked1[:, i, :], 1, i, whole)
+        interleave(early[0][:, quarter[3]], picked1[:, :, quarter[0]])
+        interleave(early[1][:, : 3 * QUARTER], picked1[:, :, QUARTER:])
         w4_scale = sb("w4_scale", [P, PASSES, M], U8, "plane0_1")
         nc.gpsimd.memset(w4_scale[:].rearrange("p a n -> p (a n)").bitcast(I32), 0)
         load_scales(nc.gpsimd, w4_scale, w4_scales)
 
-        acc = [psum.tile([P, QUARTER], F32, name=f"acc{q}") for q in range(4)]
-        gather(picked[LAST][:, 0, :], LAST, 0, 0, S)
-        quantize(mx_tiles("early_first", LAST * QUARTER), 0, early_first[:], [(0, 0), (1, 0)])
-        products(0, 0, start=True)
+        acc = [psum.tile([P, QUARTER], F32, name=f"acc{q}") for q in range(3)]
+        gather(picked2[:, 2 * HALF : 4 * HALF], LAST, WHOLE, whole)
+        quantize("early0", early[0][:], [(0, 0), (0, 1), (0, 2), (1, 0)])
+        products(0, 0)
         products(0, 1)
-        gather(picked[LAST][:, 1, :], LAST, 1, 0, S)
+        products(1, 0)
+        products(2, 0)
+        for i in (LATEST, LATE, FINAL):
+            gather(first_half[:, i, :], LAST, i, half[0])
+        gather(second_half[:, 1, 0, :], LAST, FINAL, half[1])
+        gather(second_half[:, 1, 1, :], LAST, LATE, half[1])
         for q in range(2):
-            interleave(last_a[q][:, :, 0:2], picked[LAST][:, 0:2, quarter[2 + q]])
-        gather(tail_a[:, 0, :], LAST, 2, HALF, HALF)
-        gather(tail_a[:, 1, :], LAST, 3, HALF, HALF)
-        for q in range(2):
-            interleave(last_a[q][:, :, 2:4], tail_a[:, :, quarter[q]])
-        gather(picked[LAST][:, 3, quarter[0]], LAST, 3, 0, QUARTER)
-        gather(picked[LAST][:, 2, :HALF], LAST, 2, 0, HALF)
-        last_q2 = sb("last_q2", [P, QUARTER, PACK], BF16)
-        interleave(last_q2[:], picked[LAST][:, :, quarter[0]])
-        quantize(mx_tiles("last0", QUARTER), 0, last_a[0][:], [(LAST, 0)])
-        gather(picked[LAST][:, 3, quarter[1]], LAST, 3, QUARTER, QUARTER)
-        products(0, LAST, stop=True)
-        nc.scalar.copy(out=y_sb[0][:], in_=acc[0][:])
-        warm = psum.tile([P, HALF], F32, name="warm")
-        for n in range(2):
-            nc.tensor.matmul_mx(
-                out=warm[:, quarter[n]],
-                lhsT=r8_sb[:, LAST, :].bitcast(FP8X4),
-                lhsT_scale=r8_scale[:, LAST, :],
-                rhs=operand[LAST, 0][0].bitcast(FP8X4),
-                rhs_scale=operand[LAST, 0][1],
-                start=True,
-                stop=True,
-            )
-        rest_tiles = mx_tiles("early_rest", 6 * QUARTER, "last_q0")
-        quantize(rest_tiles, 0, early_rest[:, : 3 * QUARTER], [(0, 1), (1, 1), (0, 2)])
-        quantize(mx_tiles("last1", QUARTER), 0, last_a[1][:], [(LAST, 1)])
-        quantize(rest_tiles, 3 * QUARTER, early_rest[:, 3 * QUARTER :], [(0, 3), (1, 2), (1, 3)])
-        products(1, 0, start=True)
+            interleave(last[q][:], first_half[:, :, quarter[q]])
+        quantize("last0", last[0][:], [(LAST, 0)])
+        products(0, LAST)
+        gather(second_half[:, 0, 0, quarter[0]], LAST, LATEST, quarter[2])
+        quantize("early1", early[1][:], [(1, 1), (1, 2), (1, 3), (0, 3)], "last0")
         products(1, 1)
-        products(1, LAST, stop=True)
-        nc.scalar.copy(out=y_sb[1][:], in_=acc[1][:])
-        products(2, 0, start=True)
+        quantize("last1", last[1][:], [(LAST, 1)])
+        products(1, LAST)
         products(2, 1)
-        products(3, 0, start=True)
+        gather(second_half[:, 0, 0, quarter[1]], LAST, LATEST, quarter[3])
+        nc.scalar.copy(out=y_first[:], in_=acc[0][:])
+        acc.append(psum.tile([P, QUARTER], F32, name="acc3", tag="acc0"))
+        products(3, 0)
         products(3, 1)
-        scatter(y_sb[0][:], FIRST[0], QUARTER)
-        last_q3 = sb("last_q3", [P, QUARTER, PACK], BF16, "codes_last0")
-        interleave(last_q3[:], picked[LAST][:, :, quarter[1]])
-        quantize(mx_tiles("last2", QUARTER, "picked2"), 0, last_q2[:], [(LAST, 2)])
-        quantize(mx_tiles("last3", QUARTER), 0, last_q3[:], [(LAST, 3)])
-        products(2, LAST, stop=True)
-        scatter(y_sb[1][:], FIRST[1], QUARTER)
-        nc.scalar.copy(out=y_sb[2][:, quarter[0]], in_=acc[2][:])
-        products(3, LAST, stop=True)
-        nc.scalar.copy(out=y_sb[2][:, quarter[1]], in_=acc[3][:])
-        scatter(y_sb[2][:], FIRST[2], HALF)
+        scatter(y_first[:], quarter[0])
+        last_rest = sb("last_rest", [P, HALF, PACK], BF16, "codes_last0")
+        for q in range(2):
+            interleave_second(q)
+        nc.scalar.copy(out=y_second, in_=acc[1][:])
+        for q in range(2):
+            quantize(f"last{2 + q}", last_rest[:, quarter[q]], [(LAST, 2 + q)])
+        scatter(y_second, quarter[1])
+        for q in (2, 3):
+            products(q, LAST)
+            nc.scalar.copy(out=y_rest[:, quarter[q - 2]], in_=acc[q][:])
+        scatter(y_rest[:], half[1])
         nc.sync.dma_start(out=out, in_=out_sb[:])

from contextlib import ExitStack

import concourse.mybir as mybir
from concourse.masks import make_identity

K, M, T, S = 1536, 128, 1024, 512
FLOPS = 2 * 2 * K * M * S

F32 = mybir.dt.float32
BF16 = mybir.dt.bfloat16
I32 = mybir.dt.int32
U32 = mybir.dt.uint32
U16 = mybir.dt.uint16
U8 = mybir.dt.uint8
FP8X4 = mybir.dt.float8_e4m3fn_x4
FP4X4 = mybir.dt.float4_e2m1fn_x4
MULT = mybir.AluOpType.mult
COPY = mybir.ActivationFunctionType.Copy

P = 128
PACK = 4
K_PASS = P * PACK
PASSES = K // K_PASS
LAST = PASSES - 1
HALF = S // 2
QUARTER = S // 4
LIST_ROWS = 16
GROUPS = P // LIST_ROWS
CHUNKS = S // P
WHOLE, LATEST, LATE, FINAL = 1, 0, 3, 2


def tile_list_hboth_none_kernel(
    tc, xT, w4_words, w4_scales, r8_words, r8_scales, wgt, wgo, offs, offs2, out
):
    nc = tc.nc
    with ExitStack() as ctx:
        keep = ctx.enter_context(tc.tile_pool(name="keep", bufs=1))
        psum = ctx.enter_context(tc.psum_pool(name="psum", bufs=1))

        def sb(name, shape, dtype, tag=None):
            return keep.tile(shape, dtype, name=name, tag=tag or name, align_bytes=256)

        quarter = [slice(q * QUARTER, (q + 1) * QUARTER) for q in range(4)]
        half = [slice(h * HALF, (h + 1) * HALF) for h in range(2)]

        gather_list = keep.tile([P, S // LIST_ROWS], U16, name="gather_list")
        scatter_list = keep.tile([P, S // LIST_ROWS], U16, name="scatter_list")
        planes = [[sb(f"plane{a}_{i}", [P, T], F32) for i in range(PACK)] for a in range(PASSES)]
        raw = sb("raw", [P, 2, S], F32)
        picked0 = sb("picked0", [P, 2, S], F32)
        picked1 = sb("picked1", [P, PACK, S], F32)
        picked2 = sb("picked2", [P, 14 * HALF], F32)
        first_half = picked2[:, : 8 * HALF].rearrange("p (i j) -> p i j", i=PACK)[:, :, :HALF]
        second_half = picked2[:].rearrange("p (u r j) -> p u r j", u=2, r=7)[:, :, 0:4:3, :]
        wgt_sb = picked2[:, 10 * HALF : 12 * HALF]
        wgo_sb = sb("wgo", [P, S], F32)
        w4_sb = sb("w4", [P, PASSES, 2 * M], U8)
        r8_sb = sb("r8", [P, PASSES, PACK * M], U8)
        r8_scale = sb("r8_scale", [P, PASSES, M], U8)
        early = [sb(f"early{n}", [P, S, PACK], BF16) for n in range(2)]
        last = [sb(f"last{q}", [P, QUARTER, PACK], BF16) for q in range(2)]
        y_first = sb("y_first", [P, QUARTER], F32)
        y_second = picked2[:, quarter[0]]
        y_rest = sb("y_rest", [P, HALF], F32)
        spread = [psum.tile([P, P], F32, name=f"spread{c}", tag=f"acc{c}") for c in range(CHUNKS)]
        wgt_rows = sb("wgt_rows", [P, P], F32)
        wgt_wide = sb("wgt_wide", [P, S], F32)
        identity = sb("identity", [P, P], F32)
        wgt_columns = sb("wgt_columns", [P, GROUPS, CHUNKS], F32)
        weighted = sb("weighted", [P, CHUNKS, P, 2], BF16)
        pairs = sb("pairs", [P, 2, S], F32)
        wgt_bank = psum.tile([P, P], F32, name="wgt_bank")
        out_sb = sb("out_sb", [P, T], F32)

        make_identity(nc, identity[:])
        nc.vector.memset(wgt_rows[32:64], 0.0)
        nc.vector.memset(wgt_rows[64:], 0.0)
        nc.vector.memset(r8_scale[:].rearrange("p a n -> p (a n)").bitcast(I32), 0)
        nc.vector.memset(out_sb[:], 0.0)

        def load_plane(a, i):
            rows = xT[a * K_PASS : (a + 1) * K_PASS, :].rearrange("(p i) t -> p i t", i=PACK)
            nc.sync.dma_start(out=planes[a][i][:], in_=rows[:, i, :])

        def load_scales(queue, tile, scales):
            for quad in range(4):
                queue.dma_start(
                    out=tile[32 * quad : 32 * quad + 4].bitcast(I32),
                    in_=scales[:, 4 * quad : 4 * quad + 4, :].rearrange("a r n -> r a n").bitcast(I32),
                )

        load_plane(0, 0)
        nc.sync.dma_start(gather_list[:], offs)
        nc.sync.dma_start(out=wgt_rows[:32], in_=wgt[0:P:LIST_ROWS, :].rearrange("g (c j) -> g c j", j=P))
        nc.tensor.transpose(wgt_bank[:], wgt_rows[:], identity[:])
        turned = wgt_bank[:, :32].rearrange("p (g c) -> p c g", c=CHUNKS)
        wide = wgt_wide[:].rearrange("p (c g r) -> p c g r", c=CHUNKS, r=LIST_ROWS)
        for c in range(CHUNKS):
            nc.scalar.copy(out=wide[:, c], in_=turned[:, c].unsqueeze(2).to_broadcast([P, GROUPS, LIST_ROWS]))
        for c in range(CHUNKS):
            nc.tensor.transpose(spread[c][:], wgt_wide[:, quarter[c]], identity[:])
            nc.scalar.copy(out=wgt_sb[:, quarter[c]], in_=spread[c][:])
        nc.scalar.copy(out=wgt_columns[:].rearrange("p g c -> p (g c)"), in_=wgt_bank[:, :32])
        for n in range(1, LAST * PACK):
            load_plane(n // PACK, n % PACK)
        for i in (WHOLE, LATEST, LATE, FINAL):
            load_plane(LAST, i)
        nc.sync.dma_start(out=r8_sb[:].bitcast(I32), in_=r8_words.rearrange("a p n i -> p a (n i)").bitcast(I32))
        nc.sync.dma_start(out=w4_sb[:].bitcast(I32), in_=w4_words.rearrange("a p n -> p a n").bitcast(I32))
        nc.sync.dma_start(scatter_list[:], offs2)
        load_scales(nc.sync, r8_scale, r8_scales)
        for h in range(2):
            nc.sync.dma_start(out=wgo_sb[:, half[h]], in_=wgo[:, half[h]])

        def list_part(lst, places):
            return lst[:, places.start // LIST_ROWS : places.stop // LIST_ROWS]

        def gather(dst, a, i, places):
            nc.vector.tensor_tensor(dst, planes[a][i][:].indirect(list_part(gather_list, places)), wgt_sb[:, places], MULT)

        def weigh(h):
            raw_bank = psum.tile([P, 2, 2, P], F32, name=f"raw_bank{h}", tag=f"acc{h}")
            back_bank = psum.tile([P, HALF], F32, name=f"back_bank{h}")
            for i in range(2):
                for c in range(2):
                    nc.tensor.transpose(raw_bank[:, c, i, :], raw[:, i, quarter[2 * h + c]], identity[:])
            for c in range(2):
                for g in range(GROUPS):
                    rows = slice(g * LIST_ROWS, (g + 1) * LIST_ROWS)
                    nc.scalar.activation(
                        out=weighted[:, 2 * h + c, rows, :],
                        in_=raw_bank[:, c, :, rows].rearrange("p i r -> p r i"),
                        func=COPY,
                        scale=wgt_columns[:, g, 2 * h + c : 2 * h + c + 1],
                    )
                words = weighted[:, 2 * h + c].rearrange("p r i -> p (r i)").bitcast(F32)
                nc.tensor.transpose(back_bank[:, quarter[c]], words, identity[:])
            nc.scalar.copy(out=pairs[:, 0, half[h]], in_=back_bank[:])

        def join(dst, places):
            words = dst.rearrange("p n i -> p (n i)").bitcast(U32).rearrange("p (c j u) -> p c u j", j=4, u=2)
            nc.scalar.copy(out=words, in_=pairs[:, :, places].bitcast(U32).rearrange("p u (c j) -> p c u j", j=4))

        def interleave(dst, src):
            nc.scalar.copy(out=dst.rearrange("p (c j) i -> p c i j", j=4), in_=src.rearrange("p i (c j) -> p c i j", j=4))

        def interleave_second(q):
            nc.scalar.copy(
                out=last_rest[:, quarter[q]].rearrange("p (c j) (u v) -> p c u v j", j=4, u=2),
                in_=second_half[:, :, :, quarter[q]].rearrange("p u v (c j) -> p c u v j", j=4),
            )

        operand = {}

        def quantize(name, grouped, keys, tag=None):
            width = len(keys) * QUARTER
            codes = sb(f"codes_{name}", [P, width], U32, tag)
            scales = sb(f"scales_{name}", [P, width], U8)
            nc.vector.quantize_mx(out=codes[:].bitcast(FP8X4), scales=scales[:], in_=grouped.rearrange("p c i -> p (c i)"))
            for n, key in enumerate(keys):
                operand[key] = (codes[:, quarter[n]], scales[:, quarter[n]])

        def products(q, a):
            codes, scales = operand[a, q]
            for n, (lhs, lhs_scale) in enumerate(
                ((r8_sb[:, a, :].bitcast(FP8X4), r8_scale), (w4_sb[:, a, :].bitcast(FP4X4), w4_scale))
            ):
                nc.tensor.matmul_mx(
                    out=acc[q][:],
                    lhsT=lhs,
                    lhsT_scale=lhs_scale[:, a, :],
                    rhs=codes.bitcast(FP8X4),
                    rhs_scale=scales,
                    start=(a, n) == (0, 0),
                    stop=(a, n) == (LAST, 1),
                )

        def scatter(values, places):
            nc.vector.tensor_tensor(out_sb[:].indirect(list_part(scatter_list, places)), values, wgo_sb[:, places], MULT)

        whole = slice(0, S)
        for i in range(2):
            nc.vector.tensor_copy(raw[:, i, :], planes[0][i][:].indirect(gather_list[:]))
        weigh(0)
        weigh(1)
        for h in range(2):
            gather(picked0[:, 0, half[h]], 0, 2, half[h])
        gather(picked0[:, 1, :], 0, 3, whole)
        interleave(pairs[:, 1, :].bitcast(BF16).rearrange("p (n i) -> p n i", i=2), picked0[:])
        join(early[0][:, : 3 * QUARTER], slice(0, 3 * QUARTER))
        join(early[1][:, quarter[3]], quarter[3])
        for i in range(PACK):
            gather(picked1[:, i, :], 1, i, whole)
        interleave(early[0][:, quarter[3]], picked1[:, :, quarter[0]])
        interleave(early[1][:, : 3 * QUARTER], picked1[:, :, QUARTER:])
        w4_scale = sb("w4_scale", [P, PASSES, M], U8, "plane0_1")
        nc.gpsimd.memset(w4_scale[:].rearrange("p a n -> p (a n)").bitcast(I32), 0)
        load_scales(nc.gpsimd, w4_scale, w4_scales)

        acc = [psum.tile([P, QUARTER], F32, name=f"acc{q}") for q in range(3)]
        gather(picked2[:, 2 * HALF : 4 * HALF], LAST, WHOLE, whole)
        quantize("early0", early[0][:], [(0, 0), (0, 1), (0, 2), (1, 0)])
        products(0, 0)
        products(0, 1)
        products(1, 0)
        products(2, 0)
        for i in (LATEST, LATE, FINAL):
            gather(first_half[:, i, :], LAST, i, half[0])
        gather(second_half[:, 1, 0, :], LAST, FINAL, half[1])
        gather(second_half[:, 1, 1, :], LAST, LATE, half[1])
        for q in range(2):
            interleave(last[q][:], first_half[:, :, quarter[q]])
        quantize("last0", last[0][:], [(LAST, 0)])
        products(0, LAST)
        gather(second_half[:, 0, 0, quarter[0]], LAST, LATEST, quarter[2])
        quantize("early1", early[1][:], [(1, 1), (1, 2), (1, 3), (0, 3)], "last0")
        products(1, 1)
        quantize("last1", last[1][:], [(LAST, 1)])
        products(1, LAST)
        products(2, 1)
        gather(second_half[:, 0, 0, quarter[1]], LAST, LATEST, quarter[3])
        nc.scalar.copy(out=y_first[:], in_=acc[0][:])
        acc.append(psum.tile([P, QUARTER], F32, name="acc3", tag="acc0"))
        products(3, 0)
        products(3, 1)
        scatter(y_first[:], quarter[0])
        last_rest = sb("last_rest", [P, HALF, PACK], BF16, "codes_last0")
        for q in range(2):
            interleave_second(q)
        nc.scalar.copy(out=y_second, in_=acc[1][:])
        for q in range(2):
            quantize(f"last{2 + q}", last_rest[:, quarter[q]], [(LAST, 2 + q)])
        scatter(y_second, quarter[1])
        for q in (2, 3):
            products(q, LAST)
            nc.scalar.copy(out=y_rest[:, quarter[q - 2]], in_=acc[q][:])
        scatter(y_rest[:], half[1])
        nc.sync.dma_start(out=out, in_=out_sb[:])
